import numpy as np
import ml_dtypes


def mxq(x, axis, fmt="e4m3"):
    dtype, down = {"e4m3": (ml_dtypes.float8_e4m3fn, 7), "e5m2": (ml_dtypes.float8_e5m2, 14)}[fmt]
    v = np.moveaxis(np.asarray(x, np.float32).astype(ml_dtypes.bfloat16).astype(np.float64), axis, -1)
    blocks = v.reshape(v.shape[:-1] + (-1, 32))
    amax = np.abs(blocks).max(-1, keepdims=True)
    byte = np.maximum(np.where(amax > 0, np.frexp(amax)[1] - 1 + 127, 0) - down, 1)
    scale = np.exp2(byte - 127.0)
    codes = (blocks / scale).astype(np.float32).astype(dtype).astype(np.float64)
    return np.moveaxis((codes * scale).reshape(v.shape), -1, axis)


WIDE = False


def mx_kscale(k):
    if not WIDE:
        return np.ones(k)
    levels = np.array([10, -10, 5, -5, 0])
    if k % 512:
        return np.exp2(np.random.permutation(np.resize(levels, k // 32))).repeat(32)
    a = np.empty((k // 512, 16))
    for p in range(k // 512):
        a[p, :8] = np.random.permutation(np.resize(levels, 8))
        for g in range(8):
            far = levels[np.abs(levels - a[p, g]) >= 10]
            a[p, g + 8] = far[np.random.randint(len(far))]
    return np.exp2(a.ravel()).repeat(32)


def f64(x):
    return np.asarray(x).astype(np.float64)


def striped(idx):
    return np.tile(idx.reshape(-1, 16).T, (8, 1)).astype(np.uint16)


def unstriped(offs):
    return offs[:16].T.reshape(-1).astype(np.int64)


E2M1 = np.array([0.0, 0.5, 1.0, 1.5, 2.0, 3.0, 4.0, 6.0, -0.0, -0.5, -1.0, -1.5, -2.0, -3.0, -4.0, -6.0])


def pack_weight(w, fmt):
    k, n = w.shape
    w = f64(np.asarray(w, np.float32).astype(ml_dtypes.bfloat16)).reshape(k // 32, 32, n)
    amax = np.abs(w).max(1)
    if fmt == "e4m3":
        byte = np.frexp(amax)[1] - 1 + 127 - 7
    else:
        mant, ex = np.frexp(amax / 6.0)
        byte = np.where(mant > 0.5, ex, ex - 1) + 127
    byte = np.clip(np.where(amax > 0, byte, 1), 1, 254)
    scaled = (w * np.exp2(127.0 - byte)[:, None, :]).reshape(k, n).astype(np.float32)
    by_word = np.ascontiguousarray(scaled.reshape(k // 512, 128, 4, n).transpose(0, 1, 3, 2))
    if fmt == "e4m3":
        words = by_word.astype(ml_dtypes.float8_e4m3fn).view(np.uint8)
    else:
        c = by_word.astype(ml_dtypes.float4_e2m1fn).view(np.uint8) & 0xF
        words = (c[..., 0::2] | (c[..., 1::2] << 4)).reshape(k // 512, 128, 2 * n)
    return np.ascontiguousarray(words), np.ascontiguousarray(byte.astype(np.uint8).reshape(k // 512, 16, n))


def unpack_weight(words, scales, fmt):
    g, _, n = scales.shape
    words = np.ascontiguousarray(words).reshape(g, 128, n, -1)
    if fmt == "e4m3":
        vals = words.view(ml_dtypes.float8_e4m3fn).astype(np.float64)
    else:
        nib = np.empty((g, 128, n, 4), np.uint8)
        nib[..., 0::2] = words & 0xF
        nib[..., 1::2] = words >> 4
        vals = E2M1[nib]
    vals = vals * np.repeat(np.exp2(scales.astype(np.float64) - 127.0), 8, axis=1)[..., None]
    return vals.transpose(0, 1, 3, 2).reshape(g * 512, n)


K, T, E, C, N = 1024, 512, 8, 128, 256


def by_expert(wq, xq):
    return np.concatenate([wq[e].T @ xq[:, e * C:(e + 1) * C] for e in range(E)], axis=1)


def setup_inputs():
    n = np.random.standard_normal
    s = mx_kscale(K)[:, None]
    first = np.random.permutation(np.repeat(np.arange(E), T // E))
    second = (first + 1 + np.random.permutation(np.repeat(np.arange(E - 1), -(-T // (E - 1)))[:T])) % E
    while np.bincount(second, minlength=E).max() != T // E:
        load = np.bincount(second, minlength=E); hi, lo = int(load.argmax()), int(load.argmin())
        t = np.flatnonzero((second == hi) & (first != lo))[0]; second[t] = lo
    slot_token = np.empty(E * C, np.int64); pos = np.empty((2, T), np.int64); fill = np.zeros(E, np.int64)
    place = np.stack([np.random.permutation(C) for _ in range(E)])
    for r, deal in enumerate((first, second)):
        for t in np.random.permutation(T):
            e = deal[t]; j = e * C + place[e, fill[e]]; fill[e] += 1; slot_token[j] = t; pos[r, t] = j
    g = np.random.uniform(0.2, 0.8, T)
    w = [pack_weight(m, "e2m1") for m in n((E, K, N)) / np.sqrt(K) / s[None]]
    return {
        "xT": (n((K, T)) * s).astype(np.float32),
        "w_words": np.stack([m[0] for m in w]),
        "w_scales": np.stack([m[1] for m in w]),
        "gate": np.stack([np.tile(g, (N, 1)), np.tile(1.0 - g, (N, 1))]).astype(np.float32),
        "offs": striped(slot_token),
        "pos1": striped(pos[0]),
        "pos2": striped(pos[1]),
    }


def reference(xT, w_words, w_scales, gate, offs, pos1, pos2):
    idx = unstriped(offs)
    w = np.stack([unpack_weight(w_words[e], w_scales[e], "e2m1") for e in range(E)])
    xq = mxq(f64(xT)[:, idx], 0, "e4m3")
    y = by_expert(w, xq)
    return f64(gate[0]) * y[:, unstriped(pos1)] + f64(gate[1]) * y[:, unstriped(pos2)]

@@ -1,0 +1,138 @@
+from contextlib import ExitStack
+
+import concourse.mybir as mybir
+
+F32 = mybir.dt.float32
+BF16 = mybir.dt.bfloat16
+I32 = mybir.dt.int32
+U32 = mybir.dt.uint32
+U16 = mybir.dt.uint16
+U8 = mybir.dt.uint8
+FP8X4 = mybir.dt.float8_e4m3fn_x4
+FP4X4 = mybir.dt.float4_e2m1fn_x4
+COPY = mybir.ActivationFunctionType.Copy
+ADD = mybir.AluOpType.add
+MULT = mybir.AluOpType.mult
+
+P = 128
+K, T, E, C, N = 1024, 512, 8, 128, 256
+S = E * C
+A = K // 512
+H = N // P
+FLOPS = 2 * K * N * S
+
+TC = 256
+W_WIDE = 1376
+W_CUT = 1024
+VEC_SHARE = (160, 160)
+CUTS = (512, 256, 128, 128)
+
+
+def tile_moe_pln_lin_none_kernel(tc, xT, w_words, w_scales, gate, offs, pos1, pos2, out):
+    nc = tc.nc
+    with ExitStack() as ctx:
+        keep = ctx.enter_context(tc.tile_pool(name="keep", bufs=1))
+        psum = ctx.enter_context(tc.psum_pool(name="psum", bufs=8))
+
+        offs_sb = keep.tile([P, S // 16], U16, name="offs_sb")
+        pos_sb = [keep.tile([P, T // 16], U16, name=f"pos{r}_sb") for r in range(2)]
+        raw = [[keep.tile([P, 4, TC], F32, name=f"raw{a}_{c}") for c in range(T // TC)] for a in range(A)]
+        xb = [[keep.tile([P, TC, 4], BF16, name=f"xb{a}_{c}", align_bytes=64) for c in range(T // TC)] for a in range(A)]
+        words_w = (W_WIDE, W_CUT)
+        xw = [keep.tile([P, words_w[a]], U32, name=f"xw{a}", align_bytes=64) for a in range(A)]
+        xs = [keep.tile([P, W_WIDE], U8, name=f"xs{a}", align_bytes=64) for a in range(A)]
+        gw = [keep.tile([P, S], U32, name=f"gw{a}", align_bytes=64) for a in range(A)]
+        gs = [keep.tile([P, S], U8, name=f"gs{a}", align_bytes=64) for a in range(A)]
+        wc = keep.tile([P, E * A, 2 * N], U8, name="wc", align_bytes=64)
+        ws = keep.tile([P, E * A, N], U8, name="ws", align_bytes=64)
+        gates = keep.tile([P, 2 * H, T], F32, name="gates")
+        y = [keep.tile([P, S], F32, name=f"y{h}") for h in range(H)]
+        prod = [[keep.tile([P, T], F32, name=f"prod{h}_{r}") for r in range(2)] for h in range(H)]
+        res = [keep.tile([P, T], F32, name=f"res{h}") for h in range(H)]
+
+        for a in range(A):
+            rows = xT[512 * a : 512 * (a + 1), :].rearrange("(p j) t -> p j t", j=4)
+            for c in range(T // TC):
+                nc.sync.dma_start(raw[a][c][:], rows[:, :, TC * c : TC * (c + 1)])
+            if a == 0:
+                nc.sync.dma_start(offs_sb[:], offs)
+        w_src = w_words.bitcast(I32).rearrange("e a p w -> p (e a) w")
+        w_dst = wc[:].bitcast(I32)
+        for half in range(2):
+            sl = slice(E * half, E * (half + 1))
+            nc.sync.dma_start(w_dst[:, sl, :], w_src[:, sl, :])
+
+        nc.vector.memset(xw[0][:, T:].bitcast(I32), 0)
+        for a in range(A):
+            nc.vector.memset(xs[a][:].bitcast(I32), 0)
+        nc.gpsimd.memset(ws[:].rearrange("p g n -> p (g n)").bitcast(I32), 0)
+        nc.vector.memset(xw[1][:, T:].bitcast(I32), 0)
+
+        s_src = w_scales.bitcast(I32).rearrange("e a (q r) n -> r q (e a) n", r=4)
+        s_dst = ws[:].bitcast(I32)
+        for r in range(4):
+            nc.sync.dma_start(s_dst[r : P : 32, :, :], s_src[r])
+        nc.sync.dma_start(pos_sb[0][:], pos1)
+        nc.sync.dma_start(pos_sb[1][:], pos2)
+        nc.sync.dma_start(gates[:], gate.rearrange("g (h p) t -> p (g h) t", p=P))
+
+        def cast_and_quantise(a, c):
+            v = VEC_SHARE[c] if a == 0 else 0
+            src = raw[a][c][:].rearrange("p j t -> p t j")
+            if v < TC:
+                nc.scalar.activation(xb[a][c][:, v:, :], src[:, v:, :], COPY)
+            if v > 0:
+                nc.vector.tensor_copy(xb[a][c][:, :v, :], src[:, :v, :])
+            cols = slice(TC * c, TC * (c + 1))
+            nc.vector.quantize_mx(
+                out=xw[a][:, cols].bitcast(FP8X4),
+                scales=xs[a][:, cols],
+                in_=xb[a][c][:].rearrange("p t j -> p (t j)"),
+            )
+
+        def product(bank, cols, e, h, a):
+            g = A * e + a
+            slots = slice(C * e, C * (e + 1))
+            nc.tensor.matmul_mx(
+                out=bank[:, cols],
+                lhsT=wc[:, g, 2 * P * h : 2 * P * (h + 1)].bitcast(FP4X4),
+                lhsT_scale=ws[:, g, P * h : P * (h + 1)],
+                rhs=gw[a][:, slots].bitcast(FP8X4),
+                rhs_scale=gs[a][:, slots],
+                start=(a == 0),
+                stop=(a == A - 1),
+            )
+
+        for c in range(T // TC):
+            cast_and_quantise(0, c)
+        nc.vector.tensor_copy(gw[0][:], xw[0][:].indirect(offs_sb[:]))
+        nc.vector.tensor_copy(gs[0][:], xs[0][:].indirect(offs_sb[:]))
+        banks = []
+        for e in range(E):
+            bank = psum.tile([P, C], F32, name="bank")
+            banks.append(bank)
+            product(bank, slice(0, C), e, 0, 0)
+
+        for c in range(T // TC):
+            cast_and_quantise(1, c)
+        nc.vector.tensor_copy(gs[1][:], xs[1][:].indirect(offs_sb[:]))
+        s0 = 0
+        for width in CUTS:
+            s1 = s0 + width
+            nc.vector.tensor_copy(gw[1][:, s0:s1], xw[1][:].indirect(offs_sb[:, s0 // 16 : s1 // 16]))
+            for e in range(s0 // C, s1 // C):
+                product(banks[e], slice(0, C), e, 0, 1)
+                nc.scalar.activation(y[0][:, C * e : C * (e + 1)], banks[e][:], COPY)
+            s0 = s1
+        for q in range(2):
+            bank = psum.tile([P, 4 * C], F32, name="bank")
+            for i in range(4):
+                for a in range(A):
+                    product(bank, slice(C * i, C * (i + 1)), 4 * q + i, 1, a)
+            nc.scalar.activation(y[1][:, 4 * C * q : 4 * C * (q + 1)], bank[:], COPY)
+
+        for h in range(H):
+            for r in range(2):
+                nc.vector.tensor_tensor(prod[h][r][:], y[h][:].indirect(pos_sb[r][:]), gates[:, H * r + h, :], MULT)
+            nc.vector.tensor_tensor(res[h][:], prod[h][0][:], prod[h][1][:], ADD)
+            nc.sync.dma_start(out[P * h : P * (h + 1), :], res[h][:])

@@ -40,12 +40,12 @@ def tile_moe_pln_lin_none_kernel(tc, xT, w_words, w_scales, gate, offs, pos1, po
         xb = [[keep.tile([P, TC, 4], BF16, name=f"xb{a}_{c}", align_bytes=64) for c in range(T // TC)] for a in range(A)]
         words_w = (W_WIDE, W_CUT)
         xw = [keep.tile([P, words_w[a]], U32, name=f"xw{a}", align_bytes=64) for a in range(A)]
-        xs = [keep.tile([P, W_WIDE], U8, name=f"xs{a}", align_bytes=64) for a in range(A)]
+        xs = keep.tile([P, W_CUT], U8, name="xs", align_bytes=64)
         gw = [keep.tile([P, S], U32, name=f"gw{a}", align_bytes=64) for a in range(A)]
         gs = [keep.tile([P, S], U8, name=f"gs{a}", align_bytes=64) for a in range(A)]
         wc = keep.tile([P, E * A, 2 * N], U8, name="wc", align_bytes=64)
         ws = keep.tile([P, E * A, N], U8, name="ws", align_bytes=64)
-        gates = keep.tile([P, 2 * H, T], F32, name="gates")
+        gates = keep.tile([P, 2, T], F32, name="gates")
         y = [keep.tile([P, S], F32, name=f"y{h}") for h in range(H)]
         prod = [[keep.tile([P, T], F32, name=f"prod{h}_{r}") for r in range(2)] for h in range(H)]
         res = [keep.tile([P, T], F32, name=f"res{h}") for h in range(H)]
@@ -63,8 +63,8 @@ def tile_moe_pln_lin_none_kernel(tc, xT, w_words, w_scales, gate, offs, pos1, po
             nc.sync.dma_start(w_dst[:, sl, :], w_src[:, sl, :])
 
         nc.vector.memset(xw[0][:, T:].bitcast(I32), 0)
-        for a in range(A):
-            nc.vector.memset(xs[a][:].bitcast(I32), 0)
+        nc.vector.memset(xs[:].bitcast(I32), 0)
+        nc.vector.memset(gs[1][:].bitcast(I32), 0)
         nc.gpsimd.memset(ws[:].rearrange("p g n -> p (g n)").bitcast(I32), 0)
         nc.vector.memset(xw[1][:, T:].bitcast(I32), 0)
 
@@ -74,7 +74,7 @@ def tile_moe_pln_lin_none_kernel(tc, xT, w_words, w_scales, gate, offs, pos1, po
             nc.sync.dma_start(s_dst[r : P : 32, :, :], s_src[r])
         nc.sync.dma_start(pos_sb[0][:], pos1)
         nc.sync.dma_start(pos_sb[1][:], pos2)
-        nc.sync.dma_start(gates[:], gate.rearrange("g (h p) t -> p (g h) t", p=P))
+        nc.sync.dma_start(gates[:], gate[:, :P, :].rearrange("g p t -> p g t"))
 
         def cast_and_quantise(a, c):
             v = VEC_SHARE[c] if a == 0 else 0
@@ -86,7 +86,7 @@ def tile_moe_pln_lin_none_kernel(tc, xT, w_words, w_scales, gate, offs, pos1, po
             cols = slice(TC * c, TC * (c + 1))
             nc.vector.quantize_mx(
                 out=xw[a][:, cols].bitcast(FP8X4),
-                scales=xs[a][:, cols],
+                scales=xs[4 * a :, cols],
                 in_=xb[a][c][:].rearrange("p t j -> p (t j)"),
             )
 
@@ -106,16 +106,21 @@ def tile_moe_pln_lin_none_kernel(tc, xT, w_words, w_scales, gate, offs, pos1, po
         for c in range(T // TC):
             cast_and_quantise(0, c)
         nc.vector.tensor_copy(gw[0][:], xw[0][:].indirect(offs_sb[:]))
-        nc.vector.tensor_copy(gs[0][:], xs[0][:].indirect(offs_sb[:]))
+        for c in range(T // TC):
+            cast_and_quantise(1, c)
+        both = gs[0][:].bitcast(I32)
+        moved = gs[1][:].bitcast(I32)
+        for half in range(2):
+            s0, s1 = half * S // 2, (half + 1) * S // 2
+            nc.vector.tensor_copy(gs[0][:, s0:s1], xs[:].indirect(offs_sb[:, s0 // 16 : s1 // 16]))
+            for q in range(4):
+                nc.sync.dma_start(moved[32 * q : 32 * q + 4, s0 // 4 : s1 // 4], both[32 * q + 4 : 32 * q + 8, s0 // 4 : s1 // 4])
         banks = []
         for e in range(E):
             bank = psum.tile([P, C], F32, name="bank")
             banks.append(bank)
             product(bank, slice(0, C), e, 0, 0)
 
-        for c in range(T // TC):
-            cast_and_quantise(1, c)
-        nc.vector.tensor_copy(gs[1][:], xs[1][:].indirect(offs_sb[:]))
         s0 = 0
         for width in CUTS:
             s1 = s0 + width
@@ -133,6 +138,6 @@ def tile_moe_pln_lin_none_kernel(tc, xT, w_words, w_scales, gate, offs, pos1, po
 
         for h in range(H):
             for r in range(2):
-                nc.vector.tensor_tensor(prod[h][r][:], y[h][:].indirect(pos_sb[r][:]), gates[:, H * r + h, :], MULT)
+                nc.vector.tensor_tensor(prod[h][r][:], y[h][:].indirect(pos_sb[r][:]), gates[:, r, :], MULT)
             nc.vector.tensor_tensor(res[h][:], prod[h][0][:], prod[h][1][:], ADD)
             nc.sync.dma_start(out[P * h : P * (h + 1), :], res[h][:])

@@ -32,7 +32,7 @@ def tile_moe_pln_lin_none_kernel(tc, xT, w_words, w_scales, gate, offs, pos1, po
     nc = tc.nc
     with ExitStack() as ctx:
         keep = ctx.enter_context(tc.tile_pool(name="keep", bufs=1))
-        psum = ctx.enter_context(tc.psum_pool(name="psum", bufs=8))
+        psum = ctx.enter_context(tc.psum_pool(name="psum", bufs=1))
 
         offs_sb = keep.tile([P, S // 16], U16, name="offs_sb")
         pos_sb = [keep.tile([P, T // 16], U16, name=f"pos{r}_sb") for r in range(2)]
@@ -45,7 +45,7 @@ def tile_moe_pln_lin_none_kernel(tc, xT, w_words, w_scales, gate, offs, pos1, po
         gs = [keep.tile([P, S], U8, name=f"gs{a}", align_bytes=64) for a in range(A)]
         wc = keep.tile([P, E * A, 2 * N], U8, name="wc", align_bytes=64)
         ws = keep.tile([P, E * A, N], U8, name="ws", align_bytes=64)
-        gates = keep.tile([P, 2, T], F32, name="gates")
+        gates = [keep.tile([P, T], F32, name=f"gate{r}") for r in range(2)]
         y = [keep.tile([P, S], F32, name=f"y{h}") for h in range(H)]
         prod = [[keep.tile([P, T], F32, name=f"prod{h}_{r}") for r in range(2)] for h in range(H)]
         res = [keep.tile([P, T], F32, name=f"res{h}") for h in range(H)]
@@ -58,9 +58,7 @@ def tile_moe_pln_lin_none_kernel(tc, xT, w_words, w_scales, gate, offs, pos1, po
                 nc.sync.dma_start(offs_sb[:], offs)
         w_src = w_words.bitcast(I32).rearrange("e a p w -> p (e a) w")
         w_dst = wc[:].bitcast(I32)
-        for half in range(2):
-            sl = slice(E * half, E * (half + 1))
-            nc.sync.dma_start(w_dst[:, sl, :], w_src[:, sl, :])
+        nc.sync.dma_start(w_dst[:, :E, :], w_src[:, :E, :])
 
         nc.vector.memset(xw[0][:, T:].bitcast(I32), 0)
         nc.vector.memset(xs[:].bitcast(I32), 0)
@@ -72,9 +70,7 @@ def tile_moe_pln_lin_none_kernel(tc, xT, w_words, w_scales, gate, offs, pos1, po
         s_dst = ws[:].bitcast(I32)
         for r in range(4):
             nc.sync.dma_start(s_dst[r : P : 32, :, :], s_src[r])
-        nc.sync.dma_start(pos_sb[0][:], pos1)
-        nc.sync.dma_start(pos_sb[1][:], pos2)
-        nc.sync.dma_start(gates[:], gate[:, :P, :].rearrange("g p t -> p g t"))
+        nc.sync.dma_start(w_dst[:, E:, :], w_src[:, E:, :])
 
         def cast_and_quantise(a, c):
             v = VEC_SHARE[c] if a == 0 else 0
@@ -113,11 +109,14 @@ def tile_moe_pln_lin_none_kernel(tc, xT, w_words, w_scales, gate, offs, pos1, po
         for half in range(2):
             s0, s1 = half * S // 2, (half + 1) * S // 2
             nc.vector.tensor_copy(gs[0][:, s0:s1], xs[:].indirect(offs_sb[:, s0 // 16 : s1 // 16]))
-            for q in range(4):
-                nc.sync.dma_start(moved[32 * q : 32 * q + 4, s0 // 4 : s1 // 4], both[32 * q + 4 : 32 * q + 8, s0 // 4 : s1 // 4])
+            for p0, rows in ((0, 64), (64, 4), (96, 4)):
+                nc.sync.dma_start(moved[p0 : p0 + rows, s0 // 4 : s1 // 4], both[p0 + 4 : p0 + 4 + rows, s0 // 4 : s1 // 4])
+        for r, pos in enumerate((pos1, pos2)):
+            nc.sync.dma_start(gates[r][:], gate[r, :P, :])
+            nc.sync.dma_start(pos_sb[r][:], pos)
         banks = []
         for e in range(E):
-            bank = psum.tile([P, C], F32, name="bank")
+            bank = psum.tile([P, 4 * C], F32, name=f"bank{e}")
             banks.append(bank)
             product(bank, slice(0, C), e, 0, 0)
 
@@ -127,10 +126,10 @@ def tile_moe_pln_lin_none_kernel(tc, xT, w_words, w_scales, gate, offs, pos1, po
             nc.vector.tensor_copy(gw[1][:, s0:s1], xw[1][:].indirect(offs_sb[:, s0 // 16 : s1 // 16]))
             for e in range(s0 // C, s1 // C):
                 product(banks[e], slice(0, C), e, 0, 1)
-                nc.scalar.activation(y[0][:, C * e : C * (e + 1)], banks[e][:], COPY)
+                nc.scalar.activation(y[0][:, C * e : C * (e + 1)], banks[e][:, :C], COPY)
             s0 = s1
         for q in range(2):
-            bank = psum.tile([P, 4 * C], F32, name="bank")
+            bank = psum.tile([P, 4 * C], F32, name=f"bank{E - 2 + q}")
             for i in range(4):
                 for a in range(A):
                     product(bank, slice(C * i, C * (i + 1)), 4 * q + i, 1, a)
@@ -138,6 +137,6 @@ def tile_moe_pln_lin_none_kernel(tc, xT, w_words, w_scales, gate, offs, pos1, po
 
         for h in range(H):
             for r in range(2):
-                nc.vector.tensor_tensor(prod[h][r][:], y[h][:].indirect(pos_sb[r][:]), gates[:, r, :], MULT)
+                nc.vector.tensor_tensor(prod[h][r][:], y[h][:].indirect(pos_sb[r][:]), gates[r][:], MULT)
             nc.vector.tensor_tensor(res[h][:], prod[h][0][:], prod[h][1][:], ADD)
             nc.sync.dma_start(out[P * h : P * (h + 1), :], res[h][:])

@@ -59,6 +59,7 @@ def tile_moe_pln_lin_none_kernel(tc, xT, w_words, w_scales, gate, offs, pos1, po
         w_src = w_words.bitcast(I32).rearrange("e a p w -> p (e a) w")
         w_dst = wc[:].bitcast(I32)
         nc.sync.dma_start(w_dst[:, :E, :], w_src[:, :E, :])
+        nc.sync.dma_start(w_dst[:, E:, :], w_src[:, E:, :])
 
         nc.vector.memset(xw[0][:, T:].bitcast(I32), 0)
         nc.vector.memset(xs[:].bitcast(I32), 0)
@@ -70,7 +71,6 @@ def tile_moe_pln_lin_none_kernel(tc, xT, w_words, w_scales, gate, offs, pos1, po
         s_dst = ws[:].bitcast(I32)
         for r in range(4):
             nc.sync.dma_start(s_dst[r : P : 32, :, :], s_src[r])
-        nc.sync.dma_start(w_dst[:, E:, :], w_src[:, E:, :])
 
         def cast_and_quantise(a, c):
             v = VEC_SHARE[c] if a == 0 else 0

@@ -24,8 +24,9 @@ FLOPS = 2 * K * N * S
 TC = 256
 W_WIDE = 1376
 W_CUT = 1024
-VEC_SHARE = (160, 160)
+VEC_SHARE = 96
 CUTS = (512, 256, 128, 128)
+T_CUT = 384
 
 
 def tile_moe_pln_lin_none_kernel(tc, xT, w_words, w_scales, gate, offs, pos1, pos2, out):
@@ -36,30 +37,29 @@ def tile_moe_pln_lin_none_kernel(tc, xT, w_words, w_scales, gate, offs, pos1, po
 
         offs_sb = keep.tile([P, S // 16], U16, name="offs_sb")
         pos_sb = [keep.tile([P, T // 16], U16, name=f"pos{r}_sb") for r in range(2)]
-        raw = [[keep.tile([P, 4, TC], F32, name=f"raw{a}_{c}") for c in range(T // TC)] for a in range(A)]
+        raw0 = [keep.tile([P, 2, T], F32, name=f"raw0_{u}") for u in range(2)]
+        raw1 = [keep.tile([P, 4, TC], F32, name=f"raw1_{c}") for c in range(T // TC)]
         xb = [[keep.tile([P, TC, 4], BF16, name=f"xb{a}_{c}", align_bytes=64) for c in range(T // TC)] for a in range(A)]
         words_w = (W_WIDE, W_CUT)
         xw = [keep.tile([P, words_w[a]], U32, name=f"xw{a}", align_bytes=64) for a in range(A)]
         xs = keep.tile([P, W_CUT], U8, name="xs", align_bytes=64)
         gw = [keep.tile([P, S], U32, name=f"gw{a}", align_bytes=64) for a in range(A)]
         gs = [keep.tile([P, S], U8, name=f"gs{a}", align_bytes=64) for a in range(A)]
-        wc = keep.tile([P, E * A, 2 * N], U8, name="wc", align_bytes=64)
+        wc = [keep.tile([P, E, 2 * N], U8, name=f"wc{a}", align_bytes=64) for a in range(A)]
         ws = keep.tile([P, E * A, N], U8, name="ws", align_bytes=64)
         gates = [keep.tile([P, T], F32, name=f"gate{r}") for r in range(2)]
         y = [keep.tile([P, S], F32, name=f"y{h}") for h in range(H)]
         prod = [[keep.tile([P, T], F32, name=f"prod{h}_{r}") for r in range(2)] for h in range(H)]
         res = [keep.tile([P, T], F32, name=f"res{h}") for h in range(H)]
 
-        for a in range(A):
-            rows = xT[512 * a : 512 * (a + 1), :].rearrange("(p j) t -> p j t", j=4)
-            for c in range(T // TC):
-                nc.sync.dma_start(raw[a][c][:], rows[:, :, TC * c : TC * (c + 1)])
-            if a == 0:
-                nc.sync.dma_start(offs_sb[:], offs)
-        w_src = w_words.bitcast(I32).rearrange("e a p w -> p (e a) w")
-        w_dst = wc[:].bitcast(I32)
-        nc.sync.dma_start(w_dst[:, :E, :], w_src[:, :E, :])
-        nc.sync.dma_start(w_dst[:, E:, :], w_src[:, E:, :])
+        rows = [xT[512 * a : 512 * (a + 1), :].rearrange("(p j) t -> p j t", j=4) for a in range(A)]
+        for u in range(2):
+            nc.sync.dma_start(raw0[u][:], rows[0][:, 2 * u : 2 * u + 2, :])
+        nc.sync.dma_start(offs_sb[:], offs)
+        for c in range(T // TC):
+            nc.sync.dma_start(raw1[c][:], rows[1][:, :, TC * c : TC * (c + 1)])
+        w_src = w_words.bitcast(I32).rearrange("e a p w -> a p e w")
+        nc.sync.dma_start(wc[0][:].bitcast(I32), w_src[0])
 
         nc.vector.memset(xw[0][:, T:].bitcast(I32), 0)
         nc.vector.memset(xs[:].bitcast(I32), 0)
@@ -71,14 +71,9 @@ def tile_moe_pln_lin_none_kernel(tc, xT, w_words, w_scales, gate, offs, pos1, po
         s_dst = ws[:].bitcast(I32)
         for r in range(4):
             nc.sync.dma_start(s_dst[r : P : 32, :, :], s_src[r])
+        nc.sync.dma_start(wc[1][:].bitcast(I32), w_src[1])
 
-        def cast_and_quantise(a, c):
-            v = VEC_SHARE[c] if a == 0 else 0
-            src = raw[a][c][:].rearrange("p j t -> p t j")
-            if v < TC:
-                nc.scalar.activation(xb[a][c][:, v:, :], src[:, v:, :], COPY)
-            if v > 0:
-                nc.vector.tensor_copy(xb[a][c][:, :v, :], src[:, :v, :])
+        def quantise(a, c):
             cols = slice(TC * c, TC * (c + 1))
             nc.vector.quantize_mx(
                 out=xw[a][:, cols].bitcast(FP8X4),
@@ -91,7 +86,7 @@ def tile_moe_pln_lin_none_kernel(tc, xT, w_words, w_scales, gate, offs, pos1, po
             slots = slice(C * e, C * (e + 1))
             nc.tensor.matmul_mx(
                 out=bank[:, cols],
-                lhsT=wc[:, g, 2 * P * h : 2 * P * (h + 1)].bitcast(FP4X4),
+                lhsT=wc[a][:, e, 2 * P * h : 2 * P * (h + 1)].bitcast(FP4X4),
                 lhsT_scale=ws[:, g, P * h : P * (h + 1)],
                 rhs=gw[a][:, slots].bitcast(FP8X4),
                 rhs_scale=gs[a][:, slots],
@@ -99,11 +94,18 @@ def tile_moe_pln_lin_none_kernel(tc, xT, w_words, w_scales, gate, offs, pos1, po
                 stop=(a == A - 1),
             )
 
+        for u in range(2):
+            src = raw0[u][:].rearrange("p j t -> p t j")
+            pair = slice(2 * u, 2 * u + 2)
+            nc.scalar.activation(xb[0][1][:, VEC_SHARE:, pair], src[:, TC + VEC_SHARE :, :], COPY)
+            nc.vector.tensor_copy(xb[0][0][:, :, pair], src[:, :TC, :])
+            nc.vector.tensor_copy(xb[0][1][:, :VEC_SHARE, pair], src[:, TC : TC + VEC_SHARE, :])
         for c in range(T // TC):
-            cast_and_quantise(0, c)
+            quantise(0, c)
         nc.vector.tensor_copy(gw[0][:], xw[0][:].indirect(offs_sb[:]))
         for c in range(T // TC):
-            cast_and_quantise(1, c)
+            nc.scalar.activation(xb[1][c][:], raw1[c][:].rearrange("p j t -> p t j"), COPY)
+            quantise(1, c)
         both = gs[0][:].bitcast(I32)
         moved = gs[1][:].bitcast(I32)
         for half in range(2):
@@ -135,8 +137,12 @@ def tile_moe_pln_lin_none_kernel(tc, xT, w_words, w_scales, gate, offs, pos1, po
                     product(bank, slice(C * i, C * (i + 1)), 4 * q + i, 1, a)
             nc.scalar.activation(y[1][:, 4 * C * q : 4 * C * (q + 1)], bank[:], COPY)
 
+        parts = (slice(0, T_CUT), slice(T_CUT, T))
         for h in range(H):
-            for r in range(2):
-                nc.vector.tensor_tensor(prod[h][r][:], y[h][:].indirect(pos_sb[r][:]), gates[r][:], MULT)
-            nc.vector.tensor_tensor(res[h][:], prod[h][0][:], prod[h][1][:], ADD)
-            nc.sync.dma_start(out[P * h : P * (h + 1), :], res[h][:])
+            nc.vector.tensor_tensor(prod[h][0][:], y[h][:].indirect(pos_sb[0][:]), gates[0][:], MULT)
+            for t in parts:
+                look_up = y[h][:].indirect(pos_sb[1][:, t.start // 16 : t.stop // 16])
+                nc.vector.tensor_tensor(prod[h][1][:, t], look_up, gates[1][:, t], MULT)
+            for t in parts:
+                nc.vector.tensor_tensor(res[h][:, t], prod[h][0][:, t], prod[h][1][:, t], ADD)
+                nc.sync.dma_start(out[P * h : P * (h + 1), t], res[h][:, t])

@@ -81,7 +81,7 @@ def tile_moe_pln_lin_none_kernel(tc, xT, w_words, w_scales, gate, offs, pos1, po
                 in_=xb[a][c][:].rearrange("p t j -> p (t j)"),
             )
 
-        def product(bank, cols, e, h, a):
+        def product(bank, cols, e, h, a, first):
             g = A * e + a
             slots = slice(C * e, C * (e + 1))
             nc.tensor.matmul_mx(
@@ -90,8 +90,8 @@ def tile_moe_pln_lin_none_kernel(tc, xT, w_words, w_scales, gate, offs, pos1, po
                 lhsT_scale=ws[:, g, P * h : P * (h + 1)],
                 rhs=gw[a][:, slots].bitcast(FP8X4),
                 rhs_scale=gs[a][:, slots],
-                start=(a == 0),
-                stop=(a == A - 1),
+                start=first,
+                stop=not first,
             )
 
         for u in range(2):
@@ -120,22 +120,22 @@ def tile_moe_pln_lin_none_kernel(tc, xT, w_words, w_scales, gate, offs, pos1, po
         for e in range(E):
             bank = psum.tile([P, 4 * C], F32, name=f"bank{e}")
             banks.append(bank)
-            product(bank, slice(0, C), e, 0, 0)
+            product(bank, slice(0, C), e, 0, 0, True)
 
         s0 = 0
         for width in CUTS:
             s1 = s0 + width
             nc.vector.tensor_copy(gw[1][:, s0:s1], xw[1][:].indirect(offs_sb[:, s0 // 16 : s1 // 16]))
             for e in range(s0 // C, s1 // C):
-                product(banks[e], slice(0, C), e, 0, 1)
+                product(banks[e], slice(0, C), e, 0, 1, False)
                 nc.scalar.activation(y[0][:, C * e : C * (e + 1)], banks[e][:, :C], COPY)
             s0 = s1
-        for q in range(2):
-            bank = psum.tile([P, 4 * C], F32, name=f"bank{E - 2 + q}")
-            for i in range(4):
-                for a in range(A):
-                    product(bank, slice(C * i, C * (i + 1)), 4 * q + i, 1, a)
-            nc.scalar.activation(y[1][:, 4 * C * q : 4 * C * (q + 1)], bank[:], COPY)
+        for i in range(E):
+            e = (i + E // 2) % E
+            bank = psum.tile([P, C], F32, name=f"bank{i}")
+            product(bank, slice(0, C), e, 1, 1, True)
+            product(bank, slice(0, C), e, 1, 0, False)
+            nc.scalar.activation(y[1][:, C * e : C * (e + 1)], bank[:], COPY)
 
         parts = (slice(0, T_CUT), slice(T_CUT, T))
         for h in range(H):

@@ -24,9 +24,10 @@ FLOPS = 2 * K * N * S
 TC = 256
 W_WIDE = 1376
 W_CUT = 1024
-VEC_SHARE = 96
+VEC_LOW = 64
+VEC_HIGH = 160
 CUTS = (512, 256, 128, 128)
-T_CUT = 384
+T_CUTS = ((0, 384, 512), (0, 320, 448, 512))
 
 
 def tile_moe_pln_lin_none_kernel(tc, xT, w_words, w_scales, gate, offs, pos1, pos2, out):
@@ -37,7 +38,8 @@ def tile_moe_pln_lin_none_kernel(tc, xT, w_words, w_scales, gate, offs, pos1, po
 
         offs_sb = keep.tile([P, S // 16], U16, name="offs_sb")
         pos_sb = [keep.tile([P, T // 16], U16, name=f"pos{r}_sb") for r in range(2)]
-        raw0 = [keep.tile([P, 2, T], F32, name=f"raw0_{u}") for u in range(2)]
+        low = keep.tile([P, 2, T], F32, name="low")
+        high = [keep.tile([P, 2, TC], F32, name=f"high{c}") for c in range(T // TC)]
         raw1 = [keep.tile([P, 4, TC], F32, name=f"raw1_{c}") for c in range(T // TC)]
         xb = [[keep.tile([P, TC, 4], BF16, name=f"xb{a}_{c}", align_bytes=64) for c in range(T // TC)] for a in range(A)]
         words_w = (W_WIDE, W_CUT)
@@ -53,8 +55,9 @@ def tile_moe_pln_lin_none_kernel(tc, xT, w_words, w_scales, gate, offs, pos1, po
         res = [keep.tile([P, T], F32, name=f"res{h}") for h in range(H)]
 
         rows = [xT[512 * a : 512 * (a + 1), :].rearrange("(p j) t -> p j t", j=4) for a in range(A)]
-        for u in range(2):
-            nc.sync.dma_start(raw0[u][:], rows[0][:, 2 * u : 2 * u + 2, :])
+        nc.sync.dma_start(low[:], rows[0][:, 0:2, :])
+        for c in range(T // TC):
+            nc.sync.dma_start(high[c][:], rows[0][:, 2:4, TC * c : TC * (c + 1)])
         nc.sync.dma_start(offs_sb[:], offs)
         for c in range(T // TC):
             nc.sync.dma_start(raw1[c][:], rows[1][:, :, TC * c : TC * (c + 1)])
@@ -94,13 +97,14 @@ def tile_moe_pln_lin_none_kernel(tc, xT, w_words, w_scales, gate, offs, pos1, po
                 stop=not first,
             )
 
-        for u in range(2):
-            src = raw0[u][:].rearrange("p j t -> p t j")
-            pair = slice(2 * u, 2 * u + 2)
-            nc.scalar.activation(xb[0][1][:, VEC_SHARE:, pair], src[:, TC + VEC_SHARE :, :], COPY)
-            nc.vector.tensor_copy(xb[0][0][:, :, pair], src[:, :TC, :])
-            nc.vector.tensor_copy(xb[0][1][:, :VEC_SHARE, pair], src[:, TC : TC + VEC_SHARE, :])
+        src = low[:].rearrange("p j t -> p t j")
+        nc.scalar.activation(xb[0][1][:, VEC_LOW:, 0:2], src[:, TC + VEC_LOW :, :], COPY)
+        nc.vector.tensor_copy(xb[0][0][:, :, 0:2], src[:, :TC, :])
+        nc.vector.tensor_copy(xb[0][1][:, :VEC_LOW, 0:2], src[:, TC : TC + VEC_LOW, :])
         for c in range(T // TC):
+            src = high[c][:].rearrange("p j t -> p t j")
+            nc.scalar.activation(xb[0][c][:, VEC_HIGH:, 2:4], src[:, VEC_HIGH:, :], COPY)
+            nc.vector.tensor_copy(xb[0][c][:, :VEC_HIGH, 2:4], src[:, :VEC_HIGH, :])
             quantise(0, c)
         nc.vector.tensor_copy(gw[0][:], xw[0][:].indirect(offs_sb[:]))
         for c in range(T // TC):
@@ -137,12 +141,19 @@ def tile_moe_pln_lin_none_kernel(tc, xT, w_words, w_scales, gate, offs, pos1, po
             product(bank, slice(0, C), e, 1, 0, False)
             nc.scalar.activation(y[1][:, C * e : C * (e + 1)], bank[:], COPY)
 
-        parts = (slice(0, T_CUT), slice(T_CUT, T))
+        def look_up(h, r, t):
+            window = y[h][:].indirect(pos_sb[r][:, t.start // 16 : t.stop // 16])
+            nc.vector.tensor_tensor(prod[h][r][:, t], window, gates[r][:, t], MULT)
+
+        def add_and_store(h, t):
+            nc.vector.tensor_tensor(res[h][:, t], prod[h][0][:, t], prod[h][1][:, t], ADD)
+            nc.sync.dma_start(out[P * h : P * (h + 1), t], res[h][:, t])
+
         for h in range(H):
-            nc.vector.tensor_tensor(prod[h][0][:], y[h][:].indirect(pos_sb[0][:]), gates[0][:], MULT)
-            for t in parts:
-                look_up = y[h][:].indirect(pos_sb[1][:, t.start // 16 : t.stop // 16])
-                nc.vector.tensor_tensor(prod[h][1][:, t], look_up, gates[1][:, t], MULT)
-            for t in parts:
-                nc.vector.tensor_tensor(res[h][:, t], prod[h][0][:, t], prod[h][1][:, t], ADD)
-                nc.sync.dma_start(out[P * h : P * (h + 1), t], res[h][:, t])
+            parts = [slice(t0, t1) for t0, t1 in zip(T_CUTS[h], T_CUTS[h][1:])]
+            look_up(h, 0, slice(0, T))
+            look_up(h, 1, parts[0])
+            for before, t in zip(parts, parts[1:]):
+                look_up(h, 1, t)
+                add_and_store(h, before)
+            add_and_store(h, parts[-1])

@@ -76,12 +76,12 @@ def tile_moe_pln_lin_none_kernel(tc, xT, w_words, w_scales, gate, offs, pos1, po
             nc.sync.dma_start(s_dst[r : P : 32, :, :], s_src[r])
         nc.sync.dma_start(wc[1][:].bitcast(I32), w_src[1])
 
-        def quantise(a, c):
-            cols = slice(TC * c, TC * (c + 1))
+        def quantise(a, c, t0=0, t1=TC):
+            cols = slice(TC * c + t0, TC * c + t1)
             nc.vector.quantize_mx(
                 out=xw[a][:, cols].bitcast(FP8X4),
                 scales=xs[4 * a :, cols],
-                in_=xb[a][c][:].rearrange("p t j -> p (t j)"),
+                in_=xb[a][c][:, t0:t1, :].rearrange("p t j -> p (t j)"),
             )
 
         def product(bank, cols, e, h, a, first):
@@ -107,9 +107,13 @@ def tile_moe_pln_lin_none_kernel(tc, xT, w_words, w_scales, gate, offs, pos1, po
             nc.vector.tensor_copy(xb[0][c][:, :VEC_HIGH, 2:4], src[:, :VEC_HIGH, :])
             quantise(0, c)
         nc.vector.tensor_copy(gw[0][:], xw[0][:].indirect(offs_sb[:]))
-        for c in range(T // TC):
-            nc.scalar.activation(xb[1][c][:], raw1[c][:].rearrange("p j t -> p t j"), COPY)
-            quantise(1, c)
+        nc.scalar.activation(xb[1][0][:], raw1[0][:].rearrange("p j t -> p t j"), COPY)
+        src = raw1[1][:].rearrange("p j t -> p t j")
+        nc.scalar.activation(xb[1][1][:, : TC // 2, :], src[:, : TC // 2, :], COPY)
+        nc.vector.tensor_copy(xb[1][1][:, TC // 2 :, :], src[:, TC // 2 :, :])
+        quantise(1, 0)
+        quantise(1, 1, TC // 2, TC)
+        quantise(1, 1, 0, TC // 2)
         both = gs[0][:].bitcast(I32)
         moved = gs[1][:].bitcast(I32)
         for half in range(2):

@@ -21,13 +21,16 @@ A = K // 512
 H = N // P
 FLOPS = 2 * K * N * S
 
-TC = 256
-W_WIDE = 1376
-W_CUT = 1024
+HALF = T // 2
+QUARTER = T // 4
+WINDOW_ALL = 1376
+WINDOW_HALF = 1024
 VEC_LOW = 64
 VEC_HIGH = 160
-CUTS = (512, 256, 128, 128)
-T_CUTS = ((0, 384, 512), (0, 320, 448, 512))
+VEC_LAST = 96
+WORD_PIECES = (512, 256, 128, 128)
+TOKEN_CUTS = ((0, 384, 512), (0, 320, 448, 512))
+ROW_MOVES = ((0, 64), (64, 4), (96, 4))
 
 
 def tile_moe_pln_lin_none_kernel(tc, xT, w_words, w_scales, gate, offs, pos1, pos2, out):
@@ -39,12 +42,11 @@ def tile_moe_pln_lin_none_kernel(tc, xT, w_words, w_scales, gate, offs, pos1, po
         offs_sb = keep.tile([P, S // 16], U16, name="offs_sb")
         pos_sb = [keep.tile([P, T // 16], U16, name=f"pos{r}_sb") for r in range(2)]
         low = keep.tile([P, 2, T], F32, name="low")
-        high = [keep.tile([P, 2, TC], F32, name=f"high{c}") for c in range(T // TC)]
-        raw1 = [keep.tile([P, 4, TC], F32, name=f"raw1_{c}") for c in range(T // TC)]
-        xb = [[keep.tile([P, TC, 4], BF16, name=f"xb{a}_{c}", align_bytes=64) for c in range(T // TC)] for a in range(A)]
-        words_w = (W_WIDE, W_CUT)
-        xw = [keep.tile([P, words_w[a]], U32, name=f"xw{a}", align_bytes=64) for a in range(A)]
-        xs = keep.tile([P, W_CUT], U8, name="xs", align_bytes=64)
+        high = [keep.tile([P, 2, HALF], F32, name=f"high{c}") for c in range(2)]
+        raw1 = [keep.tile([P, 4, HALF], F32, name=f"raw1_{c}") for c in range(2)]
+        xb = [[keep.tile([P, HALF, 4], BF16, name=f"xb{a}_{c}", align_bytes=64) for c in range(2)] for a in range(A)]
+        xw = [keep.tile([P, (WINDOW_ALL, WINDOW_HALF)[a]], U32, name=f"xw{a}", align_bytes=64) for a in range(A)]
+        xs = keep.tile([P, WINDOW_HALF], U8, name="xs", align_bytes=64)
         gw = [keep.tile([P, S], U32, name=f"gw{a}", align_bytes=64) for a in range(A)]
         gs = [keep.tile([P, S], U8, name=f"gs{a}", align_bytes=64) for a in range(A)]
         wc = [keep.tile([P, E, 2 * N], U8, name=f"wc{a}", align_bytes=64) for a in range(A)]
@@ -54,13 +56,13 @@ def tile_moe_pln_lin_none_kernel(tc, xT, w_words, w_scales, gate, offs, pos1, po
         prod = [[keep.tile([P, T], F32, name=f"prod{h}_{r}") for r in range(2)] for h in range(H)]
         res = [keep.tile([P, T], F32, name=f"res{h}") for h in range(H)]
 
-        rows = [xT[512 * a : 512 * (a + 1), :].rearrange("(p j) t -> p j t", j=4) for a in range(A)]
-        nc.sync.dma_start(low[:], rows[0][:, 0:2, :])
-        for c in range(T // TC):
-            nc.sync.dma_start(high[c][:], rows[0][:, 2:4, TC * c : TC * (c + 1)])
+        x_rows = [xT[512 * a : 512 * (a + 1), :].rearrange("(p j) t -> p j t", j=4) for a in range(A)]
+        nc.sync.dma_start(low[:], x_rows[0][:, 0:2, :])
+        for c in range(2):
+            nc.sync.dma_start(high[c][:], x_rows[0][:, 2:4, HALF * c : HALF * (c + 1)])
         nc.sync.dma_start(offs_sb[:], offs)
-        for c in range(T // TC):
-            nc.sync.dma_start(raw1[c][:], rows[1][:, :, TC * c : TC * (c + 1)])
+        for c in range(2):
+            nc.sync.dma_start(raw1[c][:], x_rows[1][:, :, HALF * c : HALF * (c + 1)])
         w_src = w_words.bitcast(I32).rearrange("e a p w -> a p e w")
         nc.sync.dma_start(wc[0][:].bitcast(I32), w_src[0])
 
@@ -70,27 +72,26 @@ def tile_moe_pln_lin_none_kernel(tc, xT, w_words, w_scales, gate, offs, pos1, po
         nc.gpsimd.memset(ws[:].rearrange("p g n -> p (g n)").bitcast(I32), 0)
         nc.vector.memset(xw[1][:, T:].bitcast(I32), 0)
 
-        s_src = w_scales.bitcast(I32).rearrange("e a (q r) n -> r q (e a) n", r=4)
+        s_src = w_scales.bitcast(I32).rearrange("e a (Q r) n -> r Q (e a) n", r=4)
         s_dst = ws[:].bitcast(I32)
         for r in range(4):
             nc.sync.dma_start(s_dst[r : P : 32, :, :], s_src[r])
         nc.sync.dma_start(wc[1][:].bitcast(I32), w_src[1])
 
-        def quantise(a, c, t0=0, t1=TC):
-            cols = slice(TC * c + t0, TC * c + t1)
+        def quantise(a, c, t0, t1):
+            cols = slice(HALF * c + t0, HALF * c + t1)
             nc.vector.quantize_mx(
                 out=xw[a][:, cols].bitcast(FP8X4),
                 scales=xs[4 * a :, cols],
                 in_=xb[a][c][:, t0:t1, :].rearrange("p t j -> p (t j)"),
             )
 
-        def product(bank, cols, e, h, a, first):
-            g = A * e + a
+        def product(bank, e, h, a, first):
             slots = slice(C * e, C * (e + 1))
             nc.tensor.matmul_mx(
-                out=bank[:, cols],
+                out=bank[:],
                 lhsT=wc[a][:, e, 2 * P * h : 2 * P * (h + 1)].bitcast(FP4X4),
-                lhsT_scale=ws[:, g, P * h : P * (h + 1)],
+                lhsT_scale=ws[:, A * e + a, P * h : P * (h + 1)],
                 rhs=gw[a][:, slots].bitcast(FP8X4),
                 rhs_scale=gs[a][:, slots],
                 start=first,
@@ -98,63 +99,65 @@ def tile_moe_pln_lin_none_kernel(tc, xT, w_words, w_scales, gate, offs, pos1, po
             )
 
         src = low[:].rearrange("p j t -> p t j")
-        nc.scalar.activation(xb[0][1][:, VEC_LOW:, 0:2], src[:, TC + VEC_LOW :, :], COPY)
-        nc.vector.tensor_copy(xb[0][0][:, :, 0:2], src[:, :TC, :])
-        nc.vector.tensor_copy(xb[0][1][:, :VEC_LOW, 0:2], src[:, TC : TC + VEC_LOW, :])
-        for c in range(T // TC):
+        nc.scalar.activation(xb[0][1][:, VEC_LOW:, 0:2], src[:, HALF + VEC_LOW :, :], COPY)
+        nc.vector.tensor_copy(xb[0][0][:, :, 0:2], src[:, :HALF, :])
+        nc.vector.tensor_copy(xb[0][1][:, :VEC_LOW, 0:2], src[:, HALF : HALF + VEC_LOW, :])
+        for c in range(2):
             src = high[c][:].rearrange("p j t -> p t j")
             nc.scalar.activation(xb[0][c][:, VEC_HIGH:, 2:4], src[:, VEC_HIGH:, :], COPY)
             nc.vector.tensor_copy(xb[0][c][:, :VEC_HIGH, 2:4], src[:, :VEC_HIGH, :])
-            quantise(0, c)
+            quantise(0, c, 0, HALF)
         nc.vector.tensor_copy(gw[0][:], xw[0][:].indirect(offs_sb[:]))
+
         nc.scalar.activation(xb[1][0][:], raw1[0][:].rearrange("p j t -> p t j"), COPY)
         src = raw1[1][:].rearrange("p j t -> p t j")
-        nc.scalar.activation(xb[1][1][:, : TC // 2, :], src[:, : TC // 2, :], COPY)
-        nc.vector.tensor_copy(xb[1][1][:, TC // 2 :, :], src[:, TC // 2 :, :])
-        quantise(1, 0)
-        quantise(1, 1, TC // 2, TC)
-        quantise(1, 1, 0, TC // 2)
+        for t in (slice(0, QUARTER), slice(QUARTER, HALF - VEC_LAST)):
+            nc.scalar.activation(xb[1][1][:, t, :], src[:, t, :], COPY)
+        nc.vector.tensor_copy(xb[1][1][:, HALF - VEC_LAST :, :], src[:, HALF - VEC_LAST :, :])
+        quantise(1, 0, 0, HALF)
+        quantise(1, 1, 0, QUARTER)
+        quantise(1, 1, QUARTER, HALF)
+
         both = gs[0][:].bitcast(I32)
         moved = gs[1][:].bitcast(I32)
-        for half in range(2):
-            s0, s1 = half * S // 2, (half + 1) * S // 2
+        for s0, s1 in ((0, S // 2), (S // 2, S)):
             nc.vector.tensor_copy(gs[0][:, s0:s1], xs[:].indirect(offs_sb[:, s0 // 16 : s1 // 16]))
-            for p0, rows in ((0, 64), (64, 4), (96, 4)):
-                nc.sync.dma_start(moved[p0 : p0 + rows, s0 // 4 : s1 // 4], both[p0 + 4 : p0 + 4 + rows, s0 // 4 : s1 // 4])
+            for p0, count in ROW_MOVES:
+                nc.sync.dma_start(moved[p0 : p0 + count, s0 // 4 : s1 // 4], both[p0 + 4 : p0 + 4 + count, s0 // 4 : s1 // 4])
+
         for r, pos in enumerate((pos1, pos2)):
             nc.sync.dma_start(gates[r][:], gate[r, :P, :])
             nc.sync.dma_start(pos_sb[r][:], pos)
-        banks = []
-        for e in range(E):
-            bank = psum.tile([P, 4 * C], F32, name=f"bank{e}")
-            banks.append(bank)
-            product(bank, slice(0, C), e, 0, 0, True)
 
+        banks = [psum.tile([P, C], F32, name=f"bank{e}") for e in range(E)]
+        for e in range(E):
+            product(banks[e], e, 0, 0, True)
         s0 = 0
-        for width in CUTS:
+        for width in WORD_PIECES:
             s1 = s0 + width
             nc.vector.tensor_copy(gw[1][:, s0:s1], xw[1][:].indirect(offs_sb[:, s0 // 16 : s1 // 16]))
             for e in range(s0 // C, s1 // C):
-                product(banks[e], slice(0, C), e, 0, 1, False)
-                nc.scalar.activation(y[0][:, C * e : C * (e + 1)], banks[e][:, :C], COPY)
+                product(banks[e], e, 0, 1, False)
+                nc.scalar.activation(y[0][:, C * e : C * (e + 1)], banks[e][:], COPY)
             s0 = s1
+
         for i in range(E):
             e = (i + E // 2) % E
             bank = psum.tile([P, C], F32, name=f"bank{i}")
-            product(bank, slice(0, C), e, 1, 1, True)
-            product(bank, slice(0, C), e, 1, 0, False)
+            product(bank, e, 1, 1, True)
+            product(bank, e, 1, 0, False)
             nc.scalar.activation(y[1][:, C * e : C * (e + 1)], bank[:], COPY)
 
         def look_up(h, r, t):
-            window = y[h][:].indirect(pos_sb[r][:, t.start // 16 : t.stop // 16])
-            nc.vector.tensor_tensor(prod[h][r][:, t], window, gates[r][:, t], MULT)
+            picked = y[h][:].indirect(pos_sb[r][:, t.start // 16 : t.stop // 16])
+            nc.vector.tensor_tensor(prod[h][r][:, t], picked, gates[r][:, t], MULT)
 
         def add_and_store(h, t):
             nc.vector.tensor_tensor(res[h][:, t], prod[h][0][:, t], prod[h][1][:, t], ADD)
             nc.sync.dma_start(out[P * h : P * (h + 1), t], res[h][:, t])
 
         for h in range(H):
-            parts = [slice(t0, t1) for t0, t1 in zip(T_CUTS[h], T_CUTS[h][1:])]
+            parts = [slice(t0, t1) for t0, t1 in zip(TOKEN_CUTS[h], TOKEN_CUTS[h][1:])]
             look_up(h, 0, slice(0, T))
             look_up(h, 1, parts[0])
             for before, t in zip(parts, parts[1:]):

@@ -109,11 +109,16 @@ def tile_moe_pln_lin_none_kernel(tc, xT, w_words, w_scales, gate, offs, pos1, po
             quantise(0, c, 0, HALF)
         nc.vector.tensor_copy(gw[0][:], xw[0][:].indirect(offs_sb[:]))
 
-        nc.scalar.activation(xb[1][0][:], raw1[0][:].rearrange("p j t -> p t j"), COPY)
-        src = raw1[1][:].rearrange("p j t -> p t j")
+        def by_fours(c, t):
+            return (
+                xb[1][c][:, t, :].rearrange("p (g i) j -> p g j i", i=4),
+                raw1[c][:, :, t].rearrange("p j (g i) -> p g j i", i=4),
+            )
+
+        nc.scalar.activation(*by_fours(0, slice(0, HALF)), COPY)
         for t in (slice(0, QUARTER), slice(QUARTER, HALF - VEC_LAST)):
-            nc.scalar.activation(xb[1][1][:, t, :], src[:, t, :], COPY)
-        nc.vector.tensor_copy(xb[1][1][:, HALF - VEC_LAST :, :], src[:, HALF - VEC_LAST :, :])
+            nc.scalar.activation(*by_fours(1, t), COPY)
+        nc.vector.tensor_copy(*by_fours(1, slice(HALF - VEC_LAST, HALF)))
         quantise(1, 0, 0, HALF)
         quantise(1, 1, 0, QUARTER)
         quantise(1, 1, QUARTER, HALF)

@@ -49,7 +49,8 @@ def tile_moe_pln_lin_none_kernel(tc, xT, w_words, w_scales, gate, offs, pos1, po
         xs = keep.tile([P, WINDOW_HALF], U8, name="xs", align_bytes=64)
         gw = [keep.tile([P, S], U32, name=f"gw{a}", align_bytes=64) for a in range(A)]
         gs = [keep.tile([P, S], U8, name=f"gs{a}", align_bytes=64) for a in range(A)]
-        wc = [keep.tile([P, E, 2 * N], U8, name=f"wc{a}", align_bytes=64) for a in range(A)]
+        wc0 = keep.tile([P, E, 2 * N], U8, name="wc0", align_bytes=64)
+        wc1 = [keep.tile([P, E // 2, 2 * N], U8, name=f"wc1_{g}", align_bytes=64) for g in range(2)]
         ws = keep.tile([P, E * A, N], U8, name="ws", align_bytes=64)
         gates = [keep.tile([P, T], F32, name=f"gate{r}") for r in range(2)]
         y = [keep.tile([P, S], F32, name=f"y{h}") for h in range(H)]
@@ -64,7 +65,7 @@ def tile_moe_pln_lin_none_kernel(tc, xT, w_words, w_scales, gate, offs, pos1, po
         for c in range(2):
             nc.sync.dma_start(raw1[c][:], x_rows[1][:, :, HALF * c : HALF * (c + 1)])
         w_src = w_words.bitcast(I32).rearrange("e a p w -> a p e w")
-        nc.sync.dma_start(wc[0][:].bitcast(I32), w_src[0])
+        nc.sync.dma_start(wc0[:].bitcast(I32), w_src[0])
 
         nc.vector.memset(xw[0][:, T:].bitcast(I32), 0)
         nc.vector.memset(xs[:].bitcast(I32), 0)
@@ -76,7 +77,7 @@ def tile_moe_pln_lin_none_kernel(tc, xT, w_words, w_scales, gate, offs, pos1, po
         s_dst = ws[:].bitcast(I32)
         for r in range(4):
             nc.sync.dma_start(s_dst[r : P : 32, :, :], s_src[r])
-        nc.sync.dma_start(wc[1][:].bitcast(I32), w_src[1])
+        nc.sync.dma_start(wc1[0][:].bitcast(I32), w_src[1][:, : E // 2, :])
 
         def quantise(a, c, t0, t1):
             cols = slice(HALF * c + t0, HALF * c + t1)
@@ -88,9 +89,10 @@ def tile_moe_pln_lin_none_kernel(tc, xT, w_words, w_scales, gate, offs, pos1, po
 
         def product(bank, e, h, a, first):
             slots = slice(C * e, C * (e + 1))
+            words = wc0[:, e, :] if a == 0 else wc1[e // (E // 2)][:, e % (E // 2), :]
             nc.tensor.matmul_mx(
                 out=bank[:],
-                lhsT=wc[a][:, e, 2 * P * h : 2 * P * (h + 1)].bitcast(FP4X4),
+                lhsT=words[:, 2 * P * h : 2 * P * (h + 1)].bitcast(FP4X4),
                 lhsT_scale=ws[:, A * e + a, P * h : P * (h + 1)],
                 rhs=gw[a][:, slots].bitcast(FP8X4),
                 rhs_scale=gs[a][:, slots],
@@ -129,6 +131,8 @@ def tile_moe_pln_lin_none_kernel(tc, xT, w_words, w_scales, gate, offs, pos1, po
             nc.vector.tensor_copy(gs[0][:, s0:s1], xs[:].indirect(offs_sb[:, s0 // 16 : s1 // 16]))
             for p0, count in ROW_MOVES:
                 nc.sync.dma_start(moved[p0 : p0 + count, s0 // 4 : s1 // 4], both[p0 + 4 : p0 + 4 + count, s0 // 4 : s1 // 4])
+            if s0 == 0:
+                nc.sync.dma_start(wc1[1][:].bitcast(I32), w_src[1][:, E // 2 :, :])
 
         for r, pos in enumerate((pos1, pos2)):
             nc.sync.dma_start(gates[r][:], gate[r, :P, :])

@@ -1,6 +1,7 @@
 from contextlib import ExitStack
 
 import concourse.mybir as mybir
+from concourse.masks import make_identity
 
 F32 = mybir.dt.float32
 BF16 = mybir.dt.bfloat16
@@ -23,13 +24,14 @@ FLOPS = 2 * K * N * S
 
 HALF = T // 2
 QUARTER = T // 4
+BLOCKS = T // P
 WINDOW_ALL = 1376
-WINDOW_HALF = 1024
+WINDOW_HALF = 704
 VEC_LOW = 64
 VEC_HIGH = 160
 VEC_LAST = 96
 WORD_PIECES = (512, 256, 128, 128)
-TOKEN_CUTS = ((0, 384, 512), (0, 320, 448, 512))
+TOKEN_CUTS = ((0, 256, 512), (0, 256, 448, 512))
 ROW_MOVES = ((0, 64), (64, 4), (96, 4))
 
 
@@ -56,6 +58,10 @@ def tile_moe_pln_lin_none_kernel(tc, xT, w_words, w_scales, gate, offs, pos1, po
         y = [keep.tile([P, S], F32, name=f"y{h}") for h in range(H)]
         prod = [[keep.tile([P, T], F32, name=f"prod{h}_{r}") for r in range(2)] for h in range(H)]
         res = [keep.tile([P, T], F32, name=f"res{h}") for h in range(H)]
+        turned = [keep.tile([P, P], F32, name=f"turned{b}") for b in range(BLOCKS)]
+        identity = keep.tile([P, P], F32, name="identity")
+        gate_rows = keep.tile([P, P], F32, name="gate_rows")
+        gate_cols = keep.tile([P, 2 * BLOCKS], F32, name="gate_cols")
 
         x_rows = [xT[512 * a : 512 * (a + 1), :].rearrange("(p j) t -> p j t", j=4) for a in range(A)]
         nc.sync.dma_start(low[:], x_rows[0][:, 0:2, :])
@@ -64,6 +70,9 @@ def tile_moe_pln_lin_none_kernel(tc, xT, w_words, w_scales, gate, offs, pos1, po
         nc.sync.dma_start(offs_sb[:], offs)
         for c in range(2):
             nc.sync.dma_start(raw1[c][:], x_rows[1][:, :, HALF * c : HALF * (c + 1)])
+        nc.vector.memset(gate_rows[:], 0.0)
+        for r in range(2):
+            nc.sync.dma_start(gate_rows[BLOCKS * r : BLOCKS * (r + 1), :], gate[r, 0, :].rearrange("(b t) -> b t", t=P))
         w_src = w_words.bitcast(I32).rearrange("e a p w -> a p e w")
         nc.sync.dma_start(wc0[:].bitcast(I32), w_src[0])
 
@@ -72,6 +81,7 @@ def tile_moe_pln_lin_none_kernel(tc, xT, w_words, w_scales, gate, offs, pos1, po
         nc.vector.memset(gs[1][:].bitcast(I32), 0)
         nc.gpsimd.memset(ws[:].rearrange("p g n -> p (g n)").bitcast(I32), 0)
         nc.vector.memset(xw[1][:, T:].bitcast(I32), 0)
+        make_identity(nc, identity[:])
 
         s_src = w_scales.bitcast(I32).rearrange("e a (Q r) n -> r Q (e a) n", r=4)
         s_dst = ws[:].bitcast(I32)
@@ -125,6 +135,16 @@ def tile_moe_pln_lin_none_kernel(tc, xT, w_words, w_scales, gate, offs, pos1, po
         quantise(1, 1, 0, QUARTER)
         quantise(1, 1, QUARTER, HALF)
 
+        turned_rows = psum.tile([P, P], F32, name=f"bank{E - 3}")
+        nc.tensor.transpose(turned_rows[:], gate_rows[:], identity[:])
+        nc.scalar.activation(gate_cols[:], turned_rows[:, : 2 * BLOCKS], COPY)
+        for r in range(2):
+            spread = psum.tile([P, T], F32, name=f"bank{E - 2 + r}")
+            for b in range(BLOCKS):
+                column = gate_cols[:, BLOCKS * r + b : BLOCKS * r + b + 1].to_broadcast([P, P])
+                nc.tensor.transpose(spread[:, P * b : P * (b + 1)], column, identity[:])
+            nc.scalar.activation(gates[r][:], spread[:], COPY)
+
         both = gs[0][:].bitcast(I32)
         moved = gs[1][:].bitcast(I32)
         for s0, s1 in ((0, S // 2), (S // 2, S)):
@@ -135,7 +155,6 @@ def tile_moe_pln_lin_none_kernel(tc, xT, w_words, w_scales, gate, offs, pos1, po
                 nc.sync.dma_start(wc1[1][:].bitcast(I32), w_src[1][:, E // 2 :, :])
 
         for r, pos in enumerate((pos1, pos2)):
-            nc.sync.dma_start(gates[r][:], gate[r, :P, :])
             nc.sync.dma_start(pos_sb[r][:], pos)
 
         banks = [psum.tile([P, C], F32, name=f"bank{e}") for e in range(E)]
@@ -165,11 +184,30 @@ def tile_moe_pln_lin_none_kernel(tc, xT, w_words, w_scales, gate, offs, pos1, po
             nc.vector.tensor_tensor(res[h][:, t], prod[h][0][:, t], prod[h][1][:, t], ADD)
             nc.sync.dma_start(out[P * h : P * (h + 1), t], res[h][:, t])
 
-        for h in range(H):
-            parts = [slice(t0, t1) for t0, t1 in zip(TOKEN_CUTS[h], TOKEN_CUTS[h][1:])]
-            look_up(h, 0, slice(0, T))
-            look_up(h, 1, parts[0])
-            for before, t in zip(parts, parts[1:]):
-                look_up(h, 1, t)
-                add_and_store(h, before)
-            add_and_store(h, parts[-1])
+        parts = [[slice(t0, t1) for t0, t1 in zip(cuts, cuts[1:])] for cuts in TOKEN_CUTS]
+
+        for i, part in enumerate(parts[0]):
+            blocks = range(part.start // P, part.stop // P)
+            sums = {b: psum.tile([P, P], F32, name=f"bank{E - 1 - b}") for b in blocks}
+            for r in range(2):
+                look_up(0, r, part)
+                for b in blocks:
+                    block = prod[0][r][:, P * b : P * (b + 1)]
+                    nc.tensor.matmul(sums[b][:], block, identity[:], start=r == 0, stop=r == 1, is_transpose=True)
+            for b in blocks:
+                nc.scalar.activation(turned[b][:], sums[b][:], COPY)
+            back = psum.tile([P, part.stop - part.start], F32, name=f"bank{i}")
+            for b in blocks:
+                nc.tensor.transpose(back[:, P * b - part.start : P * (b + 1) - part.start], turned[b][:], identity[:])
+            nc.scalar.activation(res[0][:, part], back[:], COPY)
+            nc.scalar.dma_start(out[:P, part], res[0][:, part])
+
+        first, middle, last = parts[1]
+        look_up(1, 0, first)
+        look_up(1, 1, first)
+        look_up(1, 0, slice(middle.start, last.stop))
+        add_and_store(1, first)
+        look_up(1, 1, middle)
+        look_up(1, 1, last)
+        add_and_store(1, middle)
+        add_and_store(1, last)

@@ -51,8 +51,6 @@ def tile_moe_pln_lin_none_kernel(tc, xT, w_words, w_scales, gate, offs, pos1, po
         xs = keep.tile([P, WINDOW_HALF], U8, name="xs", align_bytes=64)
         gw = [keep.tile([P, S], U32, name=f"gw{a}", align_bytes=64) for a in range(A)]
         gs = [keep.tile([P, S], U8, name=f"gs{a}", align_bytes=64) for a in range(A)]
-        wc0 = keep.tile([P, E, 2 * N], U8, name="wc0", align_bytes=64)
-        wc1 = [keep.tile([P, E // 2, 2 * N], U8, name=f"wc1_{g}", align_bytes=64) for g in range(2)]
         ws = keep.tile([P, E * A, N], U8, name="ws", align_bytes=64)
         gates = [keep.tile([P, T], F32, name=f"gate{r}") for r in range(2)]
         y = [keep.tile([P, S], F32, name=f"y{h}") for h in range(H)]
@@ -74,7 +72,18 @@ def tile_moe_pln_lin_none_kernel(tc, xT, w_words, w_scales, gate, offs, pos1, po
         for r in range(2):
             nc.sync.dma_start(gate_rows[BLOCKS * r : BLOCKS * (r + 1), :], gate[r, 0, :].rearrange("(b t) -> b t", t=P))
         w_src = w_words.bitcast(I32).rearrange("e a p w -> a p e w")
-        nc.sync.dma_start(wc0[:].bitcast(I32), w_src[0])
+        words = {}
+
+        def load_words(a, g, h0, h1):
+            tile = keep.tile([P, E // 2, 2 * P * (h1 - h0)], U8, name=f"wc{a}_{g}_{h0}", align_bytes=64)
+            experts = slice(E // 2 * g, E // 2 * (g + 1))
+            nc.sync.dma_start(tile[:].bitcast(I32), w_src[a][:, experts, P // 2 * h0 : P // 2 * h1])
+            for h in range(h0, h1):
+                for i in range(E // 2):
+                    words[a, experts.start + i, h] = tile[:, i, 2 * P * (h - h0) : 2 * P * (h - h0 + 1)]
+
+        load_words(0, 0, 0, 1)
+        load_words(0, 1, 0, 2)
 
         nc.vector.memset(xw[0][:, T:].bitcast(I32), 0)
         nc.vector.memset(xs[:].bitcast(I32), 0)
@@ -87,7 +96,7 @@ def tile_moe_pln_lin_none_kernel(tc, xT, w_words, w_scales, gate, offs, pos1, po
         s_dst = ws[:].bitcast(I32)
         for r in range(4):
             nc.sync.dma_start(s_dst[r : P : 32, :, :], s_src[r])
-        nc.sync.dma_start(wc1[0][:].bitcast(I32), w_src[1][:, : E // 2, :])
+        load_words(1, 0, 0, 1)
 
         def quantise(a, c, t0, t1):
             cols = slice(HALF * c + t0, HALF * c + t1)
@@ -99,10 +108,9 @@ def tile_moe_pln_lin_none_kernel(tc, xT, w_words, w_scales, gate, offs, pos1, po
 
         def product(bank, e, h, a, first):
             slots = slice(C * e, C * (e + 1))
-            words = wc0[:, e, :] if a == 0 else wc1[e // (E // 2)][:, e % (E // 2), :]
             nc.tensor.matmul_mx(
                 out=bank[:],
-                lhsT=words[:, 2 * P * h : 2 * P * (h + 1)].bitcast(FP4X4),
+                lhsT=words[a, e, h].bitcast(FP4X4),
                 lhsT_scale=ws[:, A * e + a, P * h : P * (h + 1)],
                 rhs=gw[a][:, slots].bitcast(FP8X4),
                 rhs_scale=gs[a][:, slots],
@@ -152,10 +160,13 @@ def tile_moe_pln_lin_none_kernel(tc, xT, w_words, w_scales, gate, offs, pos1, po
             for p0, count in ROW_MOVES:
                 nc.sync.dma_start(moved[p0 : p0 + count, s0 // 4 : s1 // 4], both[p0 + 4 : p0 + 4 + count, s0 // 4 : s1 // 4])
             if s0 == 0:
-                nc.sync.dma_start(wc1[1][:].bitcast(I32), w_src[1][:, E // 2 :, :])
+                load_words(1, 1, 0, 1)
 
         for r, pos in enumerate((pos1, pos2)):
             nc.sync.dma_start(pos_sb[r][:], pos)
+        load_words(1, 1, 1, 2)
+        load_words(1, 0, 1, 2)
+        load_words(0, 0, 1, 2)
 
         banks = [psum.tile([P, C], F32, name=f"bank{e}") for e in range(E)]
         for e in range(E):

@@ -27,9 +27,11 @@ QUARTER = T // 4
 BLOCKS = T // P
 WINDOW_ALL = 1376
 WINDOW_HALF = 704
+WINDOW_BYTES = 864
 VEC_LOW = 64
 VEC_HIGH = 160
 VEC_LAST = 96
+BYTE_CUTS = (0, 640, 1024)
 WORD_PIECES = (512, 256, 128, 128)
 TOKEN_CUTS = ((0, 256, 512), (0, 256, 448, 512))
 ROW_MOVES = ((0, 64), (64, 4), (96, 4))
@@ -48,7 +50,7 @@ def tile_moe_pln_lin_none_kernel(tc, xT, w_words, w_scales, gate, offs, pos1, po
         raw1 = [keep.tile([P, 4, HALF], F32, name=f"raw1_{c}") for c in range(2)]
         xb = [[keep.tile([P, HALF, 4], BF16, name=f"xb{a}_{c}", align_bytes=64) for c in range(2)] for a in range(A)]
         xw = [keep.tile([P, (WINDOW_ALL, WINDOW_HALF)[a]], U32, name=f"xw{a}", align_bytes=64) for a in range(A)]
-        xs = keep.tile([P, WINDOW_HALF], U8, name="xs", align_bytes=64)
+        xs = keep.tile([P, WINDOW_BYTES], U8, name="xs", align_bytes=64)
         gw = [keep.tile([P, S], U32, name=f"gw{a}", align_bytes=64) for a in range(A)]
         gs = [keep.tile([P, S], U8, name=f"gs{a}", align_bytes=64) for a in range(A)]
         ws = keep.tile([P, E * A, N], U8, name="ws", align_bytes=64)
@@ -155,7 +157,7 @@ def tile_moe_pln_lin_none_kernel(tc, xT, w_words, w_scales, gate, offs, pos1, po
 
         both = gs[0][:].bitcast(I32)
         moved = gs[1][:].bitcast(I32)
-        for s0, s1 in ((0, S // 2), (S // 2, S)):
+        for s0, s1 in zip(BYTE_CUTS, BYTE_CUTS[1:]):
             nc.vector.tensor_copy(gs[0][:, s0:s1], xs[:].indirect(offs_sb[:, s0 // 16 : s1 // 16]))
             for p0, count in ROW_MOVES:
                 nc.sync.dma_start(moved[p0 : p0 + count, s0 // 4 : s1 // 4], both[p0 + 4 : p0 + 4 + count, s0 // 4 : s1 // 4])

@@ -73,6 +73,8 @@ def tile_moe_pln_lin_none_kernel(tc, xT, w_words, w_scales, gate, offs, pos1, po
         nc.vector.memset(gate_rows[:], 0.0)
         for r in range(2):
             nc.sync.dma_start(gate_rows[BLOCKS * r : BLOCKS * (r + 1), :], gate[r, 0, :].rearrange("(b t) -> b t", t=P))
+        for r, pos in enumerate((pos1, pos2)):
+            nc.sync.dma_start(pos_sb[r][:], pos)
         w_src = w_words.bitcast(I32).rearrange("e a p w -> a p e w")
         words = {}
 
@@ -164,8 +166,6 @@ def tile_moe_pln_lin_none_kernel(tc, xT, w_words, w_scales, gate, offs, pos1, po
             if s0 == 0:
                 load_words(1, 1, 0, 1)
 
-        for r, pos in enumerate((pos1, pos2)):
-            nc.sync.dma_start(pos_sb[r][:], pos)
         load_words(1, 1, 1, 2)
         load_words(1, 0, 1, 2)
         load_words(0, 0, 1, 2)
@@ -216,11 +216,10 @@ def tile_moe_pln_lin_none_kernel(tc, xT, w_words, w_scales, gate, offs, pos1, po
             nc.scalar.dma_start(out[:P, part], res[0][:, part])
 
         first, middle, last = parts[1]
-        look_up(1, 0, first)
+        look_up(1, 0, slice(0, T))
         look_up(1, 1, first)
-        look_up(1, 0, slice(middle.start, last.stop))
-        add_and_store(1, first)
         look_up(1, 1, middle)
+        add_and_store(1, first)
         look_up(1, 1, last)
         add_and_store(1, middle)
         add_and_store(1, last)

@@ -11,7 +11,6 @@ U16 = mybir.dt.uint16
 U8 = mybir.dt.uint8
 FP8X4 = mybir.dt.float8_e4m3fn_x4
 FP4X4 = mybir.dt.float4_e2m1fn_x4
-COPY = mybir.ActivationFunctionType.Copy
 ADD = mybir.AluOpType.add
 MULT = mybir.AluOpType.mult
 
@@ -30,10 +29,11 @@ WINDOW_HALF = 704
 WINDOW_BYTES = 864
 VEC_LOW = 64
 VEC_HIGH = 160
-VEC_LAST = 96
+VEC_LAST = 72
 BYTE_CUTS = (0, 640, 1024)
+FIRST_LATE = BYTE_CUTS[1] // C
 WORD_PIECES = (512, 256, 128, 128)
-TOKEN_CUTS = ((0, 256, 512), (0, 256, 448, 512))
+TOKEN_CUTS = ((0, 256, 512), (0, 192, 384, 512))
 ROW_MOVES = ((0, 64), (64, 4), (96, 4))
 
 
@@ -123,12 +123,12 @@ def tile_moe_pln_lin_none_kernel(tc, xT, w_words, w_scales, gate, offs, pos1, po
             )
 
         src = low[:].rearrange("p j t -> p t j")
-        nc.scalar.activation(xb[0][1][:, VEC_LOW:, 0:2], src[:, HALF + VEC_LOW :, :], COPY)
+        nc.scalar.copy(xb[0][1][:, VEC_LOW:, 0:2], src[:, HALF + VEC_LOW :, :])
         nc.vector.tensor_copy(xb[0][0][:, :, 0:2], src[:, :HALF, :])
         nc.vector.tensor_copy(xb[0][1][:, :VEC_LOW, 0:2], src[:, HALF : HALF + VEC_LOW, :])
         for c in range(2):
             src = high[c][:].rearrange("p j t -> p t j")
-            nc.scalar.activation(xb[0][c][:, VEC_HIGH:, 2:4], src[:, VEC_HIGH:, :], COPY)
+            nc.scalar.copy(xb[0][c][:, VEC_HIGH:, 2:4], src[:, VEC_HIGH:, :])
             nc.vector.tensor_copy(xb[0][c][:, :VEC_HIGH, 2:4], src[:, :VEC_HIGH, :])
             quantise(0, c, 0, HALF)
         nc.vector.tensor_copy(gw[0][:], xw[0][:].indirect(offs_sb[:]))
@@ -139,9 +139,9 @@ def tile_moe_pln_lin_none_kernel(tc, xT, w_words, w_scales, gate, offs, pos1, po
                 raw1[c][:, :, t].rearrange("p j (g i) -> p g j i", i=4),
             )
 
-        nc.scalar.activation(*by_fours(0, slice(0, HALF)), COPY)
+        nc.scalar.copy(*by_fours(0, slice(0, HALF)))
         for t in (slice(0, QUARTER), slice(QUARTER, HALF - VEC_LAST)):
-            nc.scalar.activation(*by_fours(1, t), COPY)
+            nc.scalar.copy(*by_fours(1, t))
         nc.vector.tensor_copy(*by_fours(1, slice(HALF - VEC_LAST, HALF)))
         quantise(1, 0, 0, HALF)
         quantise(1, 1, 0, QUARTER)
@@ -149,13 +149,13 @@ def tile_moe_pln_lin_none_kernel(tc, xT, w_words, w_scales, gate, offs, pos1, po
 
         turned_rows = psum.tile([P, P], F32, name=f"bank{E - 3}")
         nc.tensor.transpose(turned_rows[:], gate_rows[:], identity[:])
-        nc.scalar.activation(gate_cols[:], turned_rows[:, : 2 * BLOCKS], COPY)
+        nc.scalar.copy(gate_cols[:], turned_rows[:, : 2 * BLOCKS])
         for r in range(2):
             spread = psum.tile([P, T], F32, name=f"bank{E - 2 + r}")
             for b in range(BLOCKS):
                 column = gate_cols[:, BLOCKS * r + b : BLOCKS * r + b + 1].to_broadcast([P, P])
                 nc.tensor.transpose(spread[:, P * b : P * (b + 1)], column, identity[:])
-            nc.scalar.activation(gates[r][:], spread[:], COPY)
+            nc.scalar.copy(gates[r][:], spread[:])
 
         both = gs[0][:].bitcast(I32)
         moved = gs[1][:].bitcast(I32)
@@ -179,15 +179,18 @@ def tile_moe_pln_lin_none_kernel(tc, xT, w_words, w_scales, gate, offs, pos1, po
             nc.vector.tensor_copy(gw[1][:, s0:s1], xw[1][:].indirect(offs_sb[:, s0 // 16 : s1 // 16]))
             for e in range(s0 // C, s1 // C):
                 product(banks[e], e, 0, 1, False)
-                nc.scalar.activation(y[0][:, C * e : C * (e + 1)], banks[e][:], COPY)
+                if e != FIRST_LATE:
+                    nc.scalar.copy(y[0][:, C * e : C * (e + 1)], banks[e][:])
             s0 = s1
+
+        nc.vector.tensor_copy(y[0][:, C * FIRST_LATE : C * (FIRST_LATE + 1)], banks[FIRST_LATE][:])
 
         for i in range(E):
             e = (i + E // 2) % E
             bank = psum.tile([P, C], F32, name=f"bank{i}")
             product(bank, e, 1, 1, True)
             product(bank, e, 1, 0, False)
-            nc.scalar.activation(y[1][:, C * e : C * (e + 1)], bank[:], COPY)
+            nc.scalar.copy(y[1][:, C * e : C * (e + 1)], bank[:])
 
         def look_up(h, r, t):
             picked = y[h][:].indirect(pos_sb[r][:, t.start // 16 : t.stop // 16])
@@ -208,11 +211,11 @@ def tile_moe_pln_lin_none_kernel(tc, xT, w_words, w_scales, gate, offs, pos1, po
                     block = prod[0][r][:, P * b : P * (b + 1)]
                     nc.tensor.matmul(sums[b][:], block, identity[:], start=r == 0, stop=r == 1, is_transpose=True)
             for b in blocks:
-                nc.scalar.activation(turned[b][:], sums[b][:], COPY)
+                nc.scalar.copy(turned[b][:], sums[b][:])
             back = psum.tile([P, part.stop - part.start], F32, name=f"bank{i}")
             for b in blocks:
                 nc.tensor.transpose(back[:, P * b - part.start : P * (b + 1) - part.start], turned[b][:], identity[:])
-            nc.scalar.activation(res[0][:, part], back[:], COPY)
+            nc.scalar.copy(res[0][:, part], back[:])
             nc.scalar.dma_start(out[:P, part], res[0][:, part])
 
         first, middle, last = parts[1]

@@ -182,7 +182,6 @@ def tile_moe_pln_lin_none_kernel(tc, xT, w_words, w_scales, gate, offs, pos1, po
                 if e != FIRST_LATE:
                     nc.scalar.copy(y[0][:, C * e : C * (e + 1)], banks[e][:])
             s0 = s1
-
         nc.vector.tensor_copy(y[0][:, C * FIRST_LATE : C * (FIRST_LATE + 1)], banks[FIRST_LATE][:])
 
         for i in range(E):
@@ -202,11 +201,12 @@ def tile_moe_pln_lin_none_kernel(tc, xT, w_words, w_scales, gate, offs, pos1, po
 
         parts = [[slice(t0, t1) for t0, t1 in zip(cuts, cuts[1:])] for cuts in TOKEN_CUTS]
 
+        look_up(0, 0, slice(0, T))
         for i, part in enumerate(parts[0]):
             blocks = range(part.start // P, part.stop // P)
             sums = {b: psum.tile([P, P], F32, name=f"bank{E - 1 - b}") for b in blocks}
+            look_up(0, 1, part)
             for r in range(2):
-                look_up(0, r, part)
                 for b in blocks:
                     block = prod[0][r][:, P * b : P * (b + 1)]
                     nc.tensor.matmul(sums[b][:], block, identity[:], start=r == 0, stop=r == 1, is_transpose=True)

@@ -46,8 +46,8 @@ def tile_moe_pln_lin_none_kernel(tc, xT, w_words, w_scales, gate, offs, pos1, po
         offs_sb = keep.tile([P, S // 16], U16, name="offs_sb")
         pos_sb = [keep.tile([P, T // 16], U16, name=f"pos{r}_sb") for r in range(2)]
         low = keep.tile([P, 2, T], F32, name="low")
-        high = [keep.tile([P, 2, HALF], F32, name=f"high{c}") for c in range(2)]
-        raw1 = [keep.tile([P, 4, HALF], F32, name=f"raw1_{c}") for c in range(2)]
+        high = keep.tile([P, 2, T], F32, name="high")
+        raw1 = keep.tile([P, 4, T], F32, name="raw1")
         xb = [[keep.tile([P, HALF, 4], BF16, name=f"xb{a}_{c}", align_bytes=64) for c in range(2)] for a in range(A)]
         xw = [keep.tile([P, (WINDOW_ALL, WINDOW_HALF)[a]], U32, name=f"xw{a}", align_bytes=64) for a in range(A)]
         xs = keep.tile([P, WINDOW_BYTES], U8, name="xs", align_bytes=64)
@@ -65,11 +65,15 @@ def tile_moe_pln_lin_none_kernel(tc, xT, w_words, w_scales, gate, offs, pos1, po
 
         x_rows = [xT[512 * a : 512 * (a + 1), :].rearrange("(p j) t -> p j t", j=4) for a in range(A)]
         nc.sync.dma_start(low[:], x_rows[0][:, 0:2, :])
-        for c in range(2):
-            nc.sync.dma_start(high[c][:], x_rows[0][:, 2:4, HALF * c : HALF * (c + 1)])
+        high_src = x_rows[0][:, 2:4, :].rearrange("p j t -> p (j t)")
+        high_dst = high[:].rearrange("p j t -> p (j t)")
+        for run in (slice(0, T + HALF), slice(T + HALF, 2 * T)):
+            nc.sync.dma_start(high_dst[:, run], high_src[:, run])
         nc.sync.dma_start(offs_sb[:], offs)
-        for c in range(2):
-            nc.sync.dma_start(raw1[c][:], x_rows[1][:, :, HALF * c : HALF * (c + 1)])
+        pairs_src = x_rows[1].rearrange("p (i j) t -> p i (j t)", j=2)
+        pairs_dst = raw1[:].rearrange("p (i j) t -> p i (j t)", j=2)
+        for run in (slice(0, T + HALF), slice(T + HALF, 2 * T)):
+            nc.sync.dma_start(pairs_dst[:, :, run], pairs_src[:, :, run])
         nc.vector.memset(gate_rows[:], 0.0)
         for r in range(2):
             nc.sync.dma_start(gate_rows[BLOCKS * r : BLOCKS * (r + 1), :], gate[r, 0, :].rearrange("(b t) -> b t", t=P))
@@ -127,16 +131,17 @@ def tile_moe_pln_lin_none_kernel(tc, xT, w_words, w_scales, gate, offs, pos1, po
         nc.vector.tensor_copy(xb[0][0][:, :, 0:2], src[:, :HALF, :])
         nc.vector.tensor_copy(xb[0][1][:, :VEC_LOW, 0:2], src[:, HALF : HALF + VEC_LOW, :])
         for c in range(2):
-            src = high[c][:].rearrange("p j t -> p t j")
+            src = high[:, :, HALF * c : HALF * (c + 1)].rearrange("p j t -> p t j")
             nc.scalar.copy(xb[0][c][:, VEC_HIGH:, 2:4], src[:, VEC_HIGH:, :])
             nc.vector.tensor_copy(xb[0][c][:, :VEC_HIGH, 2:4], src[:, :VEC_HIGH, :])
+        for c in range(2):
             quantise(0, c, 0, HALF)
         nc.vector.tensor_copy(gw[0][:], xw[0][:].indirect(offs_sb[:]))
 
         def by_fours(c, t):
             return (
                 xb[1][c][:, t, :].rearrange("p (g i) j -> p g j i", i=4),
-                raw1[c][:, :, t].rearrange("p j (g i) -> p g j i", i=4),
+                raw1[:, :, HALF * c + t.start : HALF * c + t.stop].rearrange("p j (g i) -> p g j i", i=4),
             )
 
         nc.scalar.copy(*by_fours(0, slice(0, HALF)))

@@ -29,7 +29,8 @@ WINDOW_HALF = 704
 WINDOW_BYTES = 864
 VEC_LOW = 64
 VEC_HIGH = 160
-VEC_LAST = 72
+EARLY = 192
+VEC_LAST = 80
 BYTE_CUTS = (0, 640, 1024)
 FIRST_LATE = BYTE_CUTS[1] // C
 WORD_PIECES = (512, 256, 128, 128)
@@ -47,7 +48,7 @@ def tile_moe_pln_lin_none_kernel(tc, xT, w_words, w_scales, gate, offs, pos1, po
         pos_sb = [keep.tile([P, T // 16], U16, name=f"pos{r}_sb") for r in range(2)]
         low = keep.tile([P, 2, T], F32, name="low")
         high = keep.tile([P, 2, T], F32, name="high")
-        raw1 = keep.tile([P, 4, T], F32, name="raw1")
+        raw1 = keep.tile([P, 4, T], F32, name="raw1", align_bytes=64)
         xb = [[keep.tile([P, HALF, 4], BF16, name=f"xb{a}_{c}", align_bytes=64) for c in range(2)] for a in range(A)]
         xw = [keep.tile([P, (WINDOW_ALL, WINDOW_HALF)[a]], U32, name=f"xw{a}", align_bytes=64) for a in range(A)]
         xs = keep.tile([P, WINDOW_BYTES], U8, name="xs", align_bytes=64)
@@ -72,7 +73,7 @@ def tile_moe_pln_lin_none_kernel(tc, xT, w_words, w_scales, gate, offs, pos1, po
         nc.sync.dma_start(offs_sb[:], offs)
         pairs_src = x_rows[1].rearrange("p (i j) t -> p i (j t)", j=2)
         pairs_dst = raw1[:].rearrange("p (i j) t -> p i (j t)", j=2)
-        for run in (slice(0, T + HALF), slice(T + HALF, 2 * T)):
+        for run in (slice(0, T + EARLY), slice(T + EARLY, 2 * T)):
             nc.sync.dma_start(pairs_dst[:, :, run], pairs_src[:, :, run])
         nc.vector.memset(gate_rows[:], 0.0)
         for r in range(2):
@@ -120,7 +121,7 @@ def tile_moe_pln_lin_none_kernel(tc, xT, w_words, w_scales, gate, offs, pos1, po
                 out=bank[:],
                 lhsT=words[a, e, h].bitcast(FP4X4),
                 lhsT_scale=ws[:, A * e + a, P * h : P * (h + 1)],
-                rhs=gw[a][:, slots].bitcast(FP8X4),
+                rhs=(gw_last[:] if (a, e) == (0, E - 1) else gw[a][:, slots]).bitcast(FP8X4),
                 rhs_scale=gs[a][:, slots],
                 start=first,
                 stop=not first,
@@ -136,7 +137,7 @@ def tile_moe_pln_lin_none_kernel(tc, xT, w_words, w_scales, gate, offs, pos1, po
             nc.vector.tensor_copy(xb[0][c][:, :VEC_HIGH, 2:4], src[:, :VEC_HIGH, :])
         for c in range(2):
             quantise(0, c, 0, HALF)
-        nc.vector.tensor_copy(gw[0][:], xw[0][:].indirect(offs_sb[:]))
+        nc.vector.tensor_copy(gw[0][:, : S - C], xw[0][:].indirect(offs_sb[:, : (S - C) // 16]))
 
         def by_fours(c, t):
             return (
@@ -144,13 +145,16 @@ def tile_moe_pln_lin_none_kernel(tc, xT, w_words, w_scales, gate, offs, pos1, po
                 raw1[:, :, HALF * c + t.start : HALF * c + t.stop].rearrange("p j (g i) -> p g j i", i=4),
             )
 
-        nc.scalar.copy(*by_fours(0, slice(0, HALF)))
+        for t in (slice(0, EARLY), slice(EARLY, HALF)):
+            nc.scalar.copy(*by_fours(0, t))
         for t in (slice(0, QUARTER), slice(QUARTER, HALF - VEC_LAST)):
             nc.scalar.copy(*by_fours(1, t))
         nc.vector.tensor_copy(*by_fours(1, slice(HALF - VEC_LAST, HALF)))
         quantise(1, 0, 0, HALF)
         quantise(1, 1, 0, QUARTER)
         quantise(1, 1, QUARTER, HALF)
+        gw_last = keep.tile([P, C], U32, name="raw1", align_bytes=64)
+        nc.vector.tensor_copy(gw_last[:], xw[0][:, :WINDOW_HALF].indirect(offs_sb[:, (S - C) // 16 :]))
 
         turned_rows = psum.tile([P, P], F32, name=f"bank{E - 3}")
         nc.tensor.transpose(turned_rows[:], gate_rows[:], identity[:])

@@ -13,6 +13,7 @@ FP8X4 = mybir.dt.float8_e4m3fn_x4
 FP4X4 = mybir.dt.float4_e2m1fn_x4
 ADD = mybir.AluOpType.add
 MULT = mybir.AluOpType.mult
+COPY = mybir.ActivationFunctionType.Copy
 
 P = 128
 K, T, E, C, N = 1024, 512, 8, 128, 256
@@ -59,7 +60,7 @@ def tile_moe_pln_lin_none_kernel(tc, xT, w_words, w_scales, gate, offs, pos1, po
         y = [keep.tile([P, S], F32, name=f"y{h}") for h in range(H)]
         prod = [[keep.tile([P, T], F32, name=f"prod{h}_{r}") for r in range(2)] for h in range(H)]
         res = [keep.tile([P, T], F32, name=f"res{h}") for h in range(H)]
-        turned = [keep.tile([P, P], F32, name=f"turned{b}") for b in range(BLOCKS)]
+        picked = [[keep.tile([P, T], F32, name=f"picked{h}_{r}") for r in range(2)] for h in range(H)]
         identity = keep.tile([P, P], F32, name="identity")
         gate_rows = keep.tile([P, P], F32, name="gate_rows")
         gate_cols = keep.tile([P, 2 * BLOCKS], F32, name="gate_cols")
@@ -115,20 +116,20 @@ def tile_moe_pln_lin_none_kernel(tc, xT, w_words, w_scales, gate, offs, pos1, po
                 in_=xb[a][c][:, t0:t1, :].rearrange("p t j -> p (t j)"),
             )
 
-        def product(bank, e, h, a, first):
+        def product(bank, e, h, a, start, stop):
             slots = slice(C * e, C * (e + 1))
             nc.tensor.matmul_mx(
-                out=bank[:],
+                out=bank,
                 lhsT=words[a, e, h].bitcast(FP4X4),
                 lhsT_scale=ws[:, A * e + a, P * h : P * (h + 1)],
                 rhs=(gw_last[:] if (a, e) == (0, E - 1) else gw[a][:, slots]).bitcast(FP8X4),
                 rhs_scale=gs[a][:, slots],
-                start=first,
-                stop=not first,
+                start=start,
+                stop=stop,
             )
 
         src = low[:].rearrange("p j t -> p t j")
-        nc.scalar.copy(xb[0][1][:, VEC_LOW:, 0:2], src[:, HALF + VEC_LOW :, :])
+        nc.scalar.activation(xb[0][1][:, VEC_LOW:, 0:2], src[:, HALF + VEC_LOW :, :], COPY)
         nc.vector.tensor_copy(xb[0][0][:, :, 0:2], src[:, :HALF, :])
         nc.vector.tensor_copy(xb[0][1][:, :VEC_LOW, 0:2], src[:, HALF : HALF + VEC_LOW, :])
         for c in range(2):
@@ -181,57 +182,57 @@ def tile_moe_pln_lin_none_kernel(tc, xT, w_words, w_scales, gate, offs, pos1, po
 
         banks = [psum.tile([P, C], F32, name=f"bank{e}") for e in range(E)]
         for e in range(E):
-            product(banks[e], e, 0, 0, True)
+            product(banks[e][:], e, 0, 0, True, False)
         s0 = 0
         for width in WORD_PIECES:
             s1 = s0 + width
             nc.vector.tensor_copy(gw[1][:, s0:s1], xw[1][:].indirect(offs_sb[:, s0 // 16 : s1 // 16]))
             for e in range(s0 // C, s1 // C):
-                product(banks[e], e, 0, 1, False)
+                product(banks[e][:], e, 0, 1, False, True)
                 if e != FIRST_LATE:
                     nc.scalar.copy(y[0][:, C * e : C * (e + 1)], banks[e][:])
             s0 = s1
         nc.vector.tensor_copy(y[0][:, C * FIRST_LATE : C * (FIRST_LATE + 1)], banks[FIRST_LATE][:])
 
-        for i in range(E):
-            e = (i + E // 2) % E
-            bank = psum.tile([P, C], F32, name=f"bank{i}")
-            product(bank, e, 1, 1, True)
-            product(bank, e, 1, 0, False)
-            nc.scalar.copy(y[1][:, C * e : C * (e + 1)], bank[:])
+        def row_tile_1():
+            for i, e0 in enumerate((E // 2, 0)):
+                bank = psum.tile([P, E // 2, C], F32, name=f"bank{i}")
+                for a in (1, 0):
+                    for j in range(E // 2):
+                        product(bank[:, j, :], e0 + j, 1, a, (a, j) == (1, 0), (a, j) == (0, E // 2 - 1))
+                nc.scalar.copy(y[1][:, C * e0 : C * (e0 + E // 2)], bank[:].rearrange("p j c -> p (j c)"))
 
-        def look_up(h, r, t):
-            picked = y[h][:].indirect(pos_sb[r][:, t.start // 16 : t.stop // 16])
-            nc.vector.tensor_tensor(prod[h][r][:, t], picked, gates[r][:, t], MULT)
+        def listed(h, r, t):
+            return y[h][:].indirect(pos_sb[r][:, t.start // 16 : t.stop // 16])
+
+        def fused(h, r, t):
+            nc.vector.tensor_tensor(prod[h][r][:, t], listed(h, r, t), gates[r][:, t], MULT)
+
+        def plain(h, r, t):
+            nc.scalar.activation(picked[h][r][:, t], listed(h, r, t), COPY)
+
+        def gated(h, r, t):
+            nc.vector.tensor_tensor(prod[h][r][:, t], picked[h][r][:, t], gates[r][:, t], MULT)
 
         def add_and_store(h, t):
             nc.vector.tensor_tensor(res[h][:, t], prod[h][0][:, t], prod[h][1][:, t], ADD)
             nc.sync.dma_start(out[P * h : P * (h + 1), t], res[h][:, t])
 
-        parts = [[slice(t0, t1) for t0, t1 in zip(cuts, cuts[1:])] for cuts in TOKEN_CUTS]
+        fused(0, 0, slice(0, T))
+        plain(0, 1, slice(0, 384))
+        row_tile_1()
+        gated(0, 1, slice(0, 384))
+        fused(0, 1, slice(384, T))
+        add_and_store(0, slice(0, 384))
+        add_and_store(0, slice(384, T))
 
-        look_up(0, 0, slice(0, T))
-        for i, part in enumerate(parts[0]):
-            blocks = range(part.start // P, part.stop // P)
-            sums = {b: psum.tile([P, P], F32, name=f"bank{E - 1 - b}") for b in blocks}
-            look_up(0, 1, part)
-            for r in range(2):
-                for b in blocks:
-                    block = prod[0][r][:, P * b : P * (b + 1)]
-                    nc.tensor.matmul(sums[b][:], block, identity[:], start=r == 0, stop=r == 1, is_transpose=True)
-            for b in blocks:
-                nc.scalar.copy(turned[b][:], sums[b][:])
-            back = psum.tile([P, part.stop - part.start], F32, name=f"bank{i}")
-            for b in blocks:
-                nc.tensor.transpose(back[:, P * b - part.start : P * (b + 1) - part.start], turned[b][:], identity[:])
-            nc.scalar.copy(res[0][:, part], back[:])
-            nc.scalar.dma_start(out[:P, part], res[0][:, part])
-
-        first, middle, last = parts[1]
-        look_up(1, 0, slice(0, T))
-        look_up(1, 1, first)
-        look_up(1, 1, middle)
-        add_and_store(1, first)
-        look_up(1, 1, last)
-        add_and_store(1, middle)
-        add_and_store(1, last)
+        plain(1, 1, slice(0, 256))
+        plain(1, 1, slice(256, T))
+        plain(1, 0, slice(384, T))
+        fused(1, 0, slice(0, 384))
+        gated(1, 1, slice(0, 256))
+        gated(1, 1, slice(256, T))
+        add_and_store(1, slice(0, 192))
+        gated(1, 0, slice(384, T))
+        add_and_store(1, slice(192, 384))
+        add_and_store(1, slice(384, T))

@@ -77,23 +77,21 @@ def tile_moe_pln_lin_none_kernel(tc, xT, w_words, w_scales, gate, offs, pos1, po
         for run in (slice(0, T + EARLY), slice(T + EARLY, 2 * T)):
             nc.sync.dma_start(pairs_dst[:, :, run], pairs_src[:, :, run])
         nc.vector.memset(gate_rows[:], 0.0)
-        for r in range(2):
-            nc.sync.dma_start(gate_rows[BLOCKS * r : BLOCKS * (r + 1), :], gate[r, 0, :].rearrange("(b t) -> b t", t=P))
+        gate_blocks = gate.rearrange("r n (b t) -> (r n b) t", t=P)
+        nc.sync.dma_start(gate_rows[: 2 * BLOCKS, :], gate_blocks[:: N + 1, :])
         for r, pos in enumerate((pos1, pos2)):
             nc.sync.dma_start(pos_sb[r][:], pos)
-        w_src = w_words.bitcast(I32).rearrange("e a p w -> a p e w")
+        w_rows = w_words.bitcast(I32).rearrange("e a p w -> p (e a) w")
         words = {}
 
-        def load_words(a, g, h0, h1):
-            tile = keep.tile([P, E // 2, 2 * P * (h1 - h0)], U8, name=f"wc{a}_{g}_{h0}", align_bytes=64)
-            experts = slice(E // 2 * g, E // 2 * (g + 1))
-            nc.sync.dma_start(tile[:].bitcast(I32), w_src[a][:, experts, P // 2 * h0 : P // 2 * h1])
-            for h in range(h0, h1):
-                for i in range(E // 2):
-                    words[a, experts.start + i, h] = tile[:, i, 2 * P * (h - h0) : 2 * P * (h - h0 + 1)]
+        def load_words(h, e0, e1):
+            tile = keep.tile([P, A * (e1 - e0), 2 * P], U8, name=f"words{h}_{e0}", align_bytes=64)
+            nc.sync.dma_start(tile[:].bitcast(I32), w_rows[:, A * e0 : A * e1, P // 2 * h : P // 2 * (h + 1)])
+            for e in range(e0, e1):
+                for a in range(A):
+                    words[a, e, h] = tile[:, A * (e - e0) + a, :]
 
-        load_words(0, 0, 0, 1)
-        load_words(0, 1, 0, 2)
+        load_words(0, 0, E // 2)
 
         nc.vector.memset(xw[0][:, T:].bitcast(I32), 0)
         nc.vector.memset(xs[:].bitcast(I32), 0)
@@ -106,7 +104,7 @@ def tile_moe_pln_lin_none_kernel(tc, xT, w_words, w_scales, gate, offs, pos1, po
         s_dst = ws[:].bitcast(I32)
         for r in range(4):
             nc.sync.dma_start(s_dst[r : P : 32, :, :], s_src[r])
-        load_words(1, 0, 0, 1)
+        load_words(0, E // 2, E)
 
         def quantise(a, c, t0, t1):
             cols = slice(HALF * c + t0, HALF * c + t1)
@@ -173,12 +171,9 @@ def tile_moe_pln_lin_none_kernel(tc, xT, w_words, w_scales, gate, offs, pos1, po
             nc.vector.tensor_copy(gs[0][:, s0:s1], xs[:].indirect(offs_sb[:, s0 // 16 : s1 // 16]))
             for p0, count in ROW_MOVES:
                 nc.sync.dma_start(moved[p0 : p0 + count, s0 // 4 : s1 // 4], both[p0 + 4 : p0 + 4 + count, s0 // 4 : s1 // 4])
-            if s0 == 0:
-                load_words(1, 1, 0, 1)
 
-        load_words(1, 1, 1, 2)
-        load_words(1, 0, 1, 2)
-        load_words(0, 0, 1, 2)
+        for e0, e1 in ((4, 8), (0, 2), (2, 4)):
+            load_words(1, e0, e1)
 
         banks = [psum.tile([P, C], F32, name=f"bank{e}") for e in range(E)]
         for e in range(E):
@@ -195,12 +190,12 @@ def tile_moe_pln_lin_none_kernel(tc, xT, w_words, w_scales, gate, offs, pos1, po
         nc.vector.tensor_copy(y[0][:, C * FIRST_LATE : C * (FIRST_LATE + 1)], banks[FIRST_LATE][:])
 
         def row_tile_1():
-            for i, e0 in enumerate((E // 2, 0)):
-                bank = psum.tile([P, E // 2, C], F32, name=f"bank{i}")
+            for i, (e0, count) in enumerate(((4, 4), (0, 2), (2, 2))):
+                bank = psum.tile([P, count, C], F32, name=f"bank{i}")
                 for a in (1, 0):
-                    for j in range(E // 2):
-                        product(bank[:, j, :], e0 + j, 1, a, (a, j) == (1, 0), (a, j) == (0, E // 2 - 1))
-                nc.scalar.copy(y[1][:, C * e0 : C * (e0 + E // 2)], bank[:].rearrange("p j c -> p (j c)"))
+                    for j in range(count):
+                        product(bank[:, j, :], e0 + j, 1, a, (a, j) == (1, 0), (a, j) == (0, count - 1))
+                nc.scalar.copy(y[1][:, C * e0 : C * (e0 + count)], bank[:].rearrange("p j c -> p (j c)"))
 
         def listed(h, r, t):
             return y[h][:].indirect(pos_sb[r][:, t.start // 16 : t.stop // 16])

@@ -84,14 +84,15 @@ def tile_moe_pln_lin_none_kernel(tc, xT, w_words, w_scales, gate, offs, pos1, po
         w_rows = w_words.bitcast(I32).rearrange("e a p w -> p (e a) w")
         words = {}
 
-        def load_words(h, e0, e1):
-            tile = keep.tile([P, A * (e1 - e0), 2 * P], U8, name=f"words{h}_{e0}", align_bytes=64)
-            nc.sync.dma_start(tile[:].bitcast(I32), w_rows[:, A * e0 : A * e1, P // 2 * h : P // 2 * (h + 1)])
+        def load_words(e0, e1, h0, h1):
+            tile = keep.tile([P, A * (e1 - e0), 2 * P * (h1 - h0)], U8, name=f"words{e0}_{h0}", align_bytes=64)
+            nc.sync.dma_start(tile[:].bitcast(I32), w_rows[:, A * e0 : A * e1, P // 2 * h0 : P // 2 * h1])
             for e in range(e0, e1):
                 for a in range(A):
-                    words[a, e, h] = tile[:, A * (e - e0) + a, :]
+                    for h in range(h0, h1):
+                        words[a, e, h] = tile[:, A * (e - e0) + a, 2 * P * (h - h0) : 2 * P * (h - h0 + 1)]
 
-        load_words(0, 0, E // 2)
+        load_words(0, E // 2, 0, 1)
 
         nc.vector.memset(xw[0][:, T:].bitcast(I32), 0)
         nc.vector.memset(xs[:].bitcast(I32), 0)
@@ -104,7 +105,8 @@ def tile_moe_pln_lin_none_kernel(tc, xT, w_words, w_scales, gate, offs, pos1, po
         s_dst = ws[:].bitcast(I32)
         for r in range(4):
             nc.sync.dma_start(s_dst[r : P : 32, :, :], s_src[r])
-        load_words(0, E // 2, E)
+        load_words(E // 2, E - 1, 0, 1)
+        load_words(E - 1, E, 0, 2)
 
         def quantise(a, c, t0, t1):
             cols = slice(HALF * c + t0, HALF * c + t1)
@@ -172,8 +174,8 @@ def tile_moe_pln_lin_none_kernel(tc, xT, w_words, w_scales, gate, offs, pos1, po
             for p0, count in ROW_MOVES:
                 nc.sync.dma_start(moved[p0 : p0 + count, s0 // 4 : s1 // 4], both[p0 + 4 : p0 + 4 + count, s0 // 4 : s1 // 4])
 
-        for e0, e1 in ((4, 8), (0, 2), (2, 4)):
-            load_words(1, e0, e1)
+        for e0, e1 in ((4, 7), (0, 2), (2, 3), (3, 4)):
+            load_words(e0, e1, 1, 2)
 
         banks = [psum.tile([P, C], F32, name=f"bank{e}") for e in range(E)]
         for e in range(E):
@@ -190,7 +192,7 @@ def tile_moe_pln_lin_none_kernel(tc, xT, w_words, w_scales, gate, offs, pos1, po
         nc.vector.tensor_copy(y[0][:, C * FIRST_LATE : C * (FIRST_LATE + 1)], banks[FIRST_LATE][:])
 
         def row_tile_1():
-            for i, (e0, count) in enumerate(((4, 4), (0, 2), (2, 2))):
+            for i, (e0, count) in enumerate(((4, 4), (0, 2), (2, 1), (3, 1))):
                 bank = psum.tile([P, count, C], F32, name=f"bank{i}")
                 for a in (1, 0):
                     for j in range(count):

@@ -30,8 +30,8 @@ WINDOW_HALF = 704
 WINDOW_BYTES = 864
 VEC_LOW = 64
 VEC_HIGH = 160
-EARLY = 192
-VEC_LAST = 80
+EARLY = 288
+POOL_LATE = 96
 BYTE_CUTS = (0, 640, 1024)
 FIRST_LATE = BYTE_CUTS[1] // C
 WORD_PIECES = (512, 256, 128, 128)
@@ -50,7 +50,7 @@ def tile_moe_pln_lin_none_kernel(tc, xT, w_words, w_scales, gate, offs, pos1, po
         low = keep.tile([P, 2, T], F32, name="low")
         high = keep.tile([P, 2, T], F32, name="high")
         raw1 = keep.tile([P, 4, T], F32, name="raw1", align_bytes=64)
-        xb = [[keep.tile([P, HALF, 4], BF16, name=f"xb{a}_{c}", align_bytes=64) for c in range(2)] for a in range(A)]
+        xb = [[keep.tile([P, HALF, 4], BF16, name=f"xb0_{c}", align_bytes=64) for c in range(2)]]
         xw = [keep.tile([P, (WINDOW_ALL, WINDOW_HALF)[a]], U32, name=f"xw{a}", align_bytes=64) for a in range(A)]
         xs = keep.tile([P, WINDOW_BYTES], U8, name="xs", align_bytes=64)
         gw = [keep.tile([P, S], U32, name=f"gw{a}", align_bytes=64) for a in range(A)]
@@ -140,20 +140,25 @@ def tile_moe_pln_lin_none_kernel(tc, xT, w_words, w_scales, gate, offs, pos1, po
             quantise(0, c, 0, HALF)
         nc.vector.tensor_copy(gw[0][:, : S - C], xw[0][:].indirect(offs_sb[:, : (S - C) // 16]))
 
-        def by_fours(c, t):
-            return (
-                xb[1][c][:, t, :].rearrange("p (g i) j -> p g j i", i=4),
-                raw1[:, :, HALF * c + t.start : HALF * c + t.stop].rearrange("p j (g i) -> p g j i", i=4),
+        xb1 = keep.tile([P, T, 4], BF16, name="xb1", align_bytes=64)
+
+        def cast_on_scalar(t):
+            nc.scalar.copy(
+                xb1[:, t, :].rearrange("p (g i) j -> p g j i", i=4), raw1[:, :, t].rearrange("p j (g i) -> p g j i", i=4)
             )
 
-        for t in (slice(0, EARLY), slice(EARLY, HALF)):
-            nc.scalar.copy(*by_fours(0, t))
-        for t in (slice(0, QUARTER), slice(QUARTER, HALF - VEC_LAST)):
-            nc.scalar.copy(*by_fours(1, t))
-        nc.vector.tensor_copy(*by_fours(1, slice(HALF - VEC_LAST, HALF)))
-        quantise(1, 0, 0, HALF)
-        quantise(1, 1, 0, QUARTER)
-        quantise(1, 1, QUARTER, HALF)
+        def cast_on_gpsimd(t):
+            nc.gpsimd.tensor_copy(xb1[:, t, :], raw1[:, :, t].rearrange("p j t -> p t j"))
+
+        cast_on_gpsimd(slice(0, EARLY // 2))
+        cast_on_scalar(slice(EARLY // 2, EARLY))
+        cast_on_gpsimd(slice(EARLY, EARLY + POOL_LATE))
+        cast_on_scalar(slice(EARLY + POOL_LATE, T))
+        for c in range(2):
+            cols = slice(HALF * c, HALF * (c + 1))
+            nc.vector.quantize_mx(
+                out=xw[1][:, cols].bitcast(FP8X4), scales=xs[4:, cols], in_=xb1[:, cols, :].rearrange("p t j -> p (t j)")
+            )
         gw_last = keep.tile([P, C], U32, name="raw1", align_bytes=64)
         nc.vector.tensor_copy(gw_last[:], xw[0][:, :WINDOW_HALF].indirect(offs_sb[:, (S - C) // 16 :]))
 

@@ -27,13 +27,13 @@ QUARTER = T // 4
 BLOCKS = T // P
 WINDOW_ALL = 1376
 WINDOW_HALF = 704
-WINDOW_BYTES = 864
+WINDOW_BYTES = 1024
 VEC_LOW = 64
 VEC_HIGH = 160
-EARLY = 288
-POOL_LATE = 96
-BYTE_CUTS = (0, 640, 1024)
-FIRST_LATE = BYTE_CUTS[1] // C
+EARLY = 320
+POOL_LATE = 80
+BYTE_CUTS = (0, 768, 1024)
+FIRST_LATE = 5
 WORD_PIECES = (512, 256, 128, 128)
 TOKEN_CUTS = ((0, 256, 512), (0, 192, 384, 512))
 ROW_MOVES = ((0, 64), (64, 4), (96, 4))
@@ -221,12 +221,12 @@ def tile_moe_pln_lin_none_kernel(tc, xT, w_words, w_scales, gate, offs, pos1, po
             nc.sync.dma_start(out[P * h : P * (h + 1), t], res[h][:, t])
 
         fused(0, 0, slice(0, T))
-        plain(0, 1, slice(0, 384))
+        plain(0, 1, slice(0, 320))
         row_tile_1()
-        gated(0, 1, slice(0, 384))
-        fused(0, 1, slice(384, T))
-        add_and_store(0, slice(0, 384))
-        add_and_store(0, slice(384, T))
+        gated(0, 1, slice(0, 320))
+        fused(0, 1, slice(320, T))
+        add_and_store(0, slice(0, 320))
+        add_and_store(0, slice(320, T))
 
         plain(1, 1, slice(0, 256))
         plain(1, 1, slice(256, T))

@@ -34,7 +34,7 @@ EARLY = 320
 POOL_LATE = 80
 BYTE_CUTS = (0, 768, 1024)
 FIRST_LATE = 5
-WORD_PIECES = (512, 256, 128, 128)
+WORD_PIECES = (512, 384, 128)
 TOKEN_CUTS = ((0, 256, 512), (0, 192, 384, 512))
 ROW_MOVES = ((0, 64), (64, 4), (96, 4))
 

@@ -34,6 +34,8 @@ EARLY = 320
 POOL_LATE = 80
 BYTE_CUTS = (0, 768, 1024)
 FIRST_LATE = 5
+GROUPS = ((0, 1), (2, 3), (4, 5), (6,), (7,))
+ON_VECTOR = (4, 5)
 WORD_PIECES = (512, 384, 128)
 TOKEN_CUTS = ((0, 256, 512), (0, 192, 384, 512))
 ROW_MOVES = ((0, 64), (64, 4), (96, 4))
@@ -162,11 +164,11 @@ def tile_moe_pln_lin_none_kernel(tc, xT, w_words, w_scales, gate, offs, pos1, po
         gw_last = keep.tile([P, C], U32, name="raw1", align_bytes=64)
         nc.vector.tensor_copy(gw_last[:], xw[0][:, :WINDOW_HALF].indirect(offs_sb[:, (S - C) // 16 :]))
 
-        turned_rows = psum.tile([P, P], F32, name=f"bank{E - 3}")
+        turned_rows = psum.tile([P, P], F32, name=f"bank{E - 1}")
         nc.tensor.transpose(turned_rows[:], gate_rows[:], identity[:])
         nc.scalar.copy(gate_cols[:], turned_rows[:, : 2 * BLOCKS])
         for r in range(2):
-            spread = psum.tile([P, T], F32, name=f"bank{E - 2 + r}")
+            spread = psum.tile([P, T], F32, name=f"bank{E - 3 + r}")
             for b in range(BLOCKS):
                 column = gate_cols[:, BLOCKS * r + b : BLOCKS * r + b + 1].to_broadcast([P, P])
                 nc.tensor.transpose(spread[:, P * b : P * (b + 1)], column, identity[:])
@@ -182,23 +184,30 @@ def tile_moe_pln_lin_none_kernel(tc, xT, w_words, w_scales, gate, offs, pos1, po
         for e0, e1 in ((4, 7), (0, 2), (2, 3), (3, 4)):
             load_words(e0, e1, 1, 2)
 
-        banks = [psum.tile([P, C], F32, name=f"bank{e}") for e in range(E)]
+        banks = {g: psum.tile([P, len(g), C], F32, name=f"bank{g[0]}") for g in GROUPS}
+        group_of = {e: g for g in GROUPS for e in g}
+
+        def copy_out(copy, g):
+            copy(y[0][:, C * g[0] : C * (g[-1] + 1)], banks[g][:].rearrange("p j c -> p (j c)"))
+
         for e in range(E):
-            product(banks[e][:], e, 0, 0, True, False)
+            g = group_of[e]
+            product(banks[g][:, e - g[0], :], e, 0, 0, e == g[0], False)
         s0 = 0
         for width in WORD_PIECES:
             s1 = s0 + width
             nc.vector.tensor_copy(gw[1][:, s0:s1], xw[1][:].indirect(offs_sb[:, s0 // 16 : s1 // 16]))
             for e in range(s0 // C, s1 // C):
-                product(banks[e][:], e, 0, 1, False, True)
-                if e != FIRST_LATE:
-                    nc.scalar.copy(y[0][:, C * e : C * (e + 1)], banks[e][:])
+                g = group_of[e]
+                product(banks[g][:, e - g[0], :], e, 0, 1, False, e == g[-1])
+                if e == g[-1] and g != ON_VECTOR:
+                    copy_out(nc.scalar.copy, g)
             s0 = s1
-        nc.vector.tensor_copy(y[0][:, C * FIRST_LATE : C * (FIRST_LATE + 1)], banks[FIRST_LATE][:])
+        copy_out(nc.vector.tensor_copy, ON_VECTOR)
 
         def row_tile_1():
             for i, (e0, count) in enumerate(((4, 4), (0, 2), (2, 1), (3, 1))):
-                bank = psum.tile([P, count, C], F32, name=f"bank{i}")
+                bank = psum.tile([P, count, C], F32, name=f"bank{(0, 2, 5, 6)[i]}")
                 for a in (1, 0):
                     for j in range(count):
                         product(bank[:, j, :], e0 + j, 1, a, (a, j) == (1, 0), (a, j) == (0, count - 1))

from contextlib import ExitStack

import concourse.mybir as mybir
from concourse.masks import make_identity

F32 = mybir.dt.float32
BF16 = mybir.dt.bfloat16
I32 = mybir.dt.int32
U32 = mybir.dt.uint32
U16 = mybir.dt.uint16
U8 = mybir.dt.uint8
FP8X4 = mybir.dt.float8_e4m3fn_x4
FP4X4 = mybir.dt.float4_e2m1fn_x4
ADD = mybir.AluOpType.add
MULT = mybir.AluOpType.mult
COPY = mybir.ActivationFunctionType.Copy

P = 128
K, T, E, C, N = 1024, 512, 8, 128, 256
S = E * C
A = K // 512
H = N // P
FLOPS = 2 * K * N * S

HALF = T // 2
QUARTER = T // 4
BLOCKS = T // P
WINDOW_ALL = 1376
WINDOW_HALF = 704
WINDOW_BYTES = 1024
VEC_LOW = 64
VEC_HIGH = 160
EARLY = 320
POOL_LATE = 80
BYTE_CUTS = (0, 768, 1024)
FIRST_LATE = 5
GROUPS = ((0, 1), (2, 3), (4, 5), (6,), (7,))
ON_VECTOR = (4, 5)
WORD_PIECES = (512, 384, 128)
TOKEN_CUTS = ((0, 256, 512), (0, 192, 384, 512))
ROW_MOVES = ((0, 64), (64, 4), (96, 4))


def tile_moe_pln_lin_none_kernel(tc, xT, w_words, w_scales, gate, offs, pos1, pos2, out):
    nc = tc.nc
    with ExitStack() as ctx:
        keep = ctx.enter_context(tc.tile_pool(name="keep", bufs=1))
        psum = ctx.enter_context(tc.psum_pool(name="psum", bufs=1))

        offs_sb = keep.tile([P, S // 16], U16, name="offs_sb")
        pos_sb = [keep.tile([P, T // 16], U16, name=f"pos{r}_sb") for r in range(2)]
        low = keep.tile([P, 2, T], F32, name="low")
        high = keep.tile([P, 2, T], F32, name="high")
        raw1 = keep.tile([P, 4, T], F32, name="raw1", align_bytes=64)
        xb = [[keep.tile([P, HALF, 4], BF16, name=f"xb0_{c}", align_bytes=64) for c in range(2)]]
        xw = [keep.tile([P, (WINDOW_ALL, WINDOW_HALF)[a]], U32, name=f"xw{a}", align_bytes=64) for a in range(A)]
        xs = keep.tile([P, WINDOW_BYTES], U8, name="xs", align_bytes=64)
        gw = [keep.tile([P, S], U32, name=f"gw{a}", align_bytes=64) for a in range(A)]
        gs = [keep.tile([P, S], U8, name=f"gs{a}", align_bytes=64) for a in range(A)]
        ws = keep.tile([P, E * A, N], U8, name="ws", align_bytes=64)
        gates = [keep.tile([P, T], F32, name=f"gate{r}") for r in range(2)]
        y = [keep.tile([P, S], F32, name=f"y{h}") for h in range(H)]
        prod = [[keep.tile([P, T], F32, name=f"prod{h}_{r}") for r in range(2)] for h in range(H)]
        res = [keep.tile([P, T], F32, name=f"res{h}") for h in range(H)]
        picked = [[keep.tile([P, T], F32, name=f"picked{h}_{r}") for r in range(2)] for h in range(H)]
        identity = keep.tile([P, P], F32, name="identity")
        gate_rows = keep.tile([P, P], F32, name="gate_rows")
        gate_cols = keep.tile([P, 2 * BLOCKS], F32, name="gate_cols")

        x_rows = [xT[512 * a : 512 * (a + 1), :].rearrange("(p j) t -> p j t", j=4) for a in range(A)]
        nc.sync.dma_start(low[:], x_rows[0][:, 0:2, :])
        high_src = x_rows[0][:, 2:4, :].rearrange("p j t -> p (j t)")
        high_dst = high[:].rearrange("p j t -> p (j t)")
        for run in (slice(0, T + HALF), slice(T + HALF, 2 * T)):
            nc.sync.dma_start(high_dst[:, run], high_src[:, run])
        nc.sync.dma_start(offs_sb[:], offs)
        pairs_src = x_rows[1].rearrange("p (i j) t -> p i (j t)", j=2)
        pairs_dst = raw1[:].rearrange("p (i j) t -> p i (j t)", j=2)
        for run in (slice(0, T + EARLY), slice(T + EARLY, 2 * T)):
            nc.sync.dma_start(pairs_dst[:, :, run], pairs_src[:, :, run])
        nc.vector.memset(gate_rows[:], 0.0)
        gate_blocks = gate.rearrange("r n (b t) -> (r n b) t", t=P)
        nc.sync.dma_start(gate_rows[: 2 * BLOCKS, :], gate_blocks[:: N + 1, :])
        for r, pos in enumerate((pos1, pos2)):
            nc.sync.dma_start(pos_sb[r][:], pos)
        w_rows = w_words.bitcast(I32).rearrange("e a p w -> p (e a) w")
        words = {}

        def load_words(e0, e1, h0, h1):
            tile = keep.tile([P, A * (e1 - e0), 2 * P * (h1 - h0)], U8, name=f"words{e0}_{h0}", align_bytes=64)
            nc.sync.dma_start(tile[:].bitcast(I32), w_rows[:, A * e0 : A * e1, P // 2 * h0 : P // 2 * h1])
            for e in range(e0, e1):
                for a in range(A):
                    for h in range(h0, h1):
                        words[a, e, h] = tile[:, A * (e - e0) + a, 2 * P * (h - h0) : 2 * P * (h - h0 + 1)]

        load_words(0, E // 2, 0, 1)

        nc.vector.memset(xw[0][:, T:].bitcast(I32), 0)
        nc.vector.memset(xs[:].bitcast(I32), 0)
        nc.vector.memset(gs[1][:].bitcast(I32), 0)
        nc.gpsimd.memset(ws[:].rearrange("p g n -> p (g n)").bitcast(I32), 0)
        nc.vector.memset(xw[1][:, T:].bitcast(I32), 0)
        make_identity(nc, identity[:])

        s_src = w_scales.bitcast(I32).rearrange("e a (Q r) n -> r Q (e a) n", r=4)
        s_dst = ws[:].bitcast(I32)
        for r in range(4):
            nc.sync.dma_start(s_dst[r : P : 32, :, :], s_src[r])
        load_words(E // 2, E - 1, 0, 1)
        load_words(E - 1, E, 0, 2)

        def quantise(a, c, t0, t1):
            cols = slice(HALF * c + t0, HALF * c + t1)
            nc.vector.quantize_mx(
                out=xw[a][:, cols].bitcast(FP8X4),
                scales=xs[4 * a :, cols],
                in_=xb[a][c][:, t0:t1, :].rearrange("p t j -> p (t j)"),
            )

        def product(bank, e, h, a, start, stop):
            slots = slice(C * e, C * (e + 1))
            nc.tensor.matmul_mx(
                out=bank,
                lhsT=words[a, e, h].bitcast(FP4X4),
                lhsT_scale=ws[:, A * e + a, P * h : P * (h + 1)],
                rhs=(gw_last[:] if (a, e) == (0, E - 1) else gw[a][:, slots]).bitcast(FP8X4),
                rhs_scale=gs[a][:, slots],
                start=start,
                stop=stop,
            )

        src = low[:].rearrange("p j t -> p t j")
        nc.scalar.activation(xb[0][1][:, VEC_LOW:, 0:2], src[:, HALF + VEC_LOW :, :], COPY)
        nc.vector.tensor_copy(xb[0][0][:, :, 0:2], src[:, :HALF, :])
        nc.vector.tensor_copy(xb[0][1][:, :VEC_LOW, 0:2], src[:, HALF : HALF + VEC_LOW, :])
        for c in range(2):
            src = high[:, :, HALF * c : HALF * (c + 1)].rearrange("p j t -> p t j")
            nc.scalar.copy(xb[0][c][:, VEC_HIGH:, 2:4], src[:, VEC_HIGH:, :])
            nc.vector.tensor_copy(xb[0][c][:, :VEC_HIGH, 2:4], src[:, :VEC_HIGH, :])
        for c in range(2):
            quantise(0, c, 0, HALF)
        nc.vector.tensor_copy(gw[0][:, : S - C], xw[0][:].indirect(offs_sb[:, : (S - C) // 16]))

        xb1 = keep.tile([P, T, 4], BF16, name="xb1", align_bytes=64)

        def cast_on_scalar(t):
            nc.scalar.copy(
                xb1[:, t, :].rearrange("p (g i) j -> p g j i", i=4), raw1[:, :, t].rearrange("p j (g i) -> p g j i", i=4)
            )

        def cast_on_gpsimd(t):
            nc.gpsimd.tensor_copy(xb1[:, t, :], raw1[:, :, t].rearrange("p j t -> p t j"))

        cast_on_gpsimd(slice(0, EARLY // 2))
        cast_on_scalar(slice(EARLY // 2, EARLY))
        cast_on_gpsimd(slice(EARLY, EARLY + POOL_LATE))
        cast_on_scalar(slice(EARLY + POOL_LATE, T))
        for c in range(2):
            cols = slice(HALF * c, HALF * (c + 1))
            nc.vector.quantize_mx(
                out=xw[1][:, cols].bitcast(FP8X4), scales=xs[4:, cols], in_=xb1[:, cols, :].rearrange("p t j -> p (t j)")
            )
        gw_last = keep.tile([P, C], U32, name="raw1", align_bytes=64)
        nc.vector.tensor_copy(gw_last[:], xw[0][:, :WINDOW_HALF].indirect(offs_sb[:, (S - C) // 16 :]))

        turned_rows = psum.tile([P, P], F32, name=f"bank{E - 1}")
        nc.tensor.transpose(turned_rows[:], gate_rows[:], identity[:])
        nc.scalar.copy(gate_cols[:], turned_rows[:, : 2 * BLOCKS])
        for r in range(2):
            spread = psum.tile([P, T], F32, name=f"bank{E - 3 + r}")
            for b in range(BLOCKS):
                column = gate_cols[:, BLOCKS * r + b : BLOCKS * r + b + 1].to_broadcast([P, P])
                nc.tensor.transpose(spread[:, P * b : P * (b + 1)], column, identity[:])
            nc.scalar.copy(gates[r][:], spread[:])

        both = gs[0][:].bitcast(I32)
        moved = gs[1][:].bitcast(I32)
        for s0, s1 in zip(BYTE_CUTS, BYTE_CUTS[1:]):
            nc.vector.tensor_copy(gs[0][:, s0:s1], xs[:].indirect(offs_sb[:, s0 // 16 : s1 // 16]))
            for p0, count in ROW_MOVES:
                nc.sync.dma_start(moved[p0 : p0 + count, s0 // 4 : s1 // 4], both[p0 + 4 : p0 + 4 + count, s0 // 4 : s1 // 4])

        for e0, e1 in ((4, 7), (0, 2), (2, 3), (3, 4)):
            load_words(e0, e1, 1, 2)

        banks = {g: psum.tile([P, len(g), C], F32, name=f"bank{g[0]}") for g in GROUPS}
        group_of = {e: g for g in GROUPS for e in g}

        def copy_out(copy, g):
            copy(y[0][:, C * g[0] : C * (g[-1] + 1)], banks[g][:].rearrange("p j c -> p (j c)"))

        for e in range(E):
            g = group_of[e]
            product(banks[g][:, e - g[0], :], e, 0, 0, e == g[0], False)
        s0 = 0
        for width in WORD_PIECES:
            s1 = s0 + width
            nc.vector.tensor_copy(gw[1][:, s0:s1], xw[1][:].indirect(offs_sb[:, s0 // 16 : s1 // 16]))
            for e in range(s0 // C, s1 // C):
                g = group_of[e]
                product(banks[g][:, e - g[0], :], e, 0, 1, False, e == g[-1])
                if e == g[-1] and g != ON_VECTOR:
                    copy_out(nc.scalar.copy, g)
            s0 = s1
        copy_out(nc.vector.tensor_copy, ON_VECTOR)

        def row_tile_1():
            for i, (e0, count) in enumerate(((4, 4), (0, 2), (2, 1), (3, 1))):
                bank = psum.tile([P, count, C], F32, name=f"bank{(0, 2, 5, 6)[i]}")
                for a in (1, 0):
                    for j in range(count):
                        product(bank[:, j, :], e0 + j, 1, a, (a, j) == (1, 0), (a, j) == (0, count - 1))
                nc.scalar.copy(y[1][:, C * e0 : C * (e0 + count)], bank[:].rearrange("p j c -> p (j c)"))

        def listed(h, r, t):
            return y[h][:].indirect(pos_sb[r][:, t.start // 16 : t.stop // 16])

        def fused(h, r, t):
            nc.vector.tensor_tensor(prod[h][r][:, t], listed(h, r, t), gates[r][:, t], MULT)

        def plain(h, r, t):
            nc.scalar.activation(picked[h][r][:, t], listed(h, r, t), COPY)

        def gated(h, r, t):
            nc.vector.tensor_tensor(prod[h][r][:, t], picked[h][r][:, t], gates[r][:, t], MULT)

        def add_and_store(h, t):
            nc.vector.tensor_tensor(res[h][:, t], prod[h][0][:, t], prod[h][1][:, t], ADD)
            nc.sync.dma_start(out[P * h : P * (h + 1), t], res[h][:, t])

        fused(0, 0, slice(0, T))
        plain(0, 1, slice(0, 320))
        row_tile_1()
        gated(0, 1, slice(0, 320))
        fused(0, 1, slice(320, T))
        add_and_store(0, slice(0, 320))
        add_and_store(0, slice(320, T))

        plain(1, 1, slice(0, 256))
        plain(1, 1, slice(256, T))
        plain(1, 0, slice(384, T))
        fused(1, 0, slice(0, 384))
        gated(1, 1, slice(0, 256))
        gated(1, 1, slice(256, T))
        add_and_store(1, slice(0, 192))
        gated(1, 0, slice(384, T))
        add_and_store(1, slice(192, 384))
        add_and_store(1, slice(384, T))
